import numpy as np, ml_dtypes
CORES = [3,11,19,27,35,43,51,59]
N = 8
import mx_ref
BF = ml_dtypes.bfloat16
def pick(q, e):
    c = np.concatenate([q[0].reshape(128, -1, 4), np.zeros((128, 1, 4), np.uint8)], axis=1); s = np.concatenate([q[1], np.ones((16, 1), np.uint8)], axis=1)
    return (np.ascontiguousarray(c[:, e].reshape(128, -1)), np.ascontiguousarray(s[:, e]))
def join(*qs):
    return (np.concatenate([q[0] for q in qs], axis=1), np.concatenate([q[1] for q in qs], axis=1))
def put(q, e, v):
    c, s = q[0].reshape(128, -1, 4).copy(), q[1].copy(); c[:, e] = v[0].reshape(128, -1, 4); s[:, e] = v[1]
    return (c.reshape(128, -1), s)
def pk(c, s):
    return (np.ascontiguousarray(c), mx_ref.live(s))
def emit(q):
    return q[0], q[1]
def decode(q):
    o = []
    for b in range(4):
        e = np.zeros((128, 128, 4), np.float32); e[np.arange(128), np.arange(128), b] = 1
        o.append(mx_ref.matmul(mx_ref.quantize(e.reshape(128, 512).astype(BF)), q))
    return np.stack(o, axis=2).reshape(128, -1)
def cut(t, i, w=512):
    return t[:, w * i:w * i + w]
def f(rng, *shape):
    return mx_ref.flush((rng.standard_normal(shape, dtype=np.float32) * np.exp2(rng.integers(-2, 3, shape[:-1] + (1,)))).astype(BF))
def wide(rng, *shape, cols=0):
    v = rng.standard_normal(shape, dtype=np.float32) * np.exp2(rng.integers(-12, 13, shape)).astype(np.float32)
    if cols: v *= np.repeat(np.exp2(rng.integers(-cols, cols + 1, shape[:-2] + (1, shape[-1] // 4))) * (rng.random(shape[:-2] + (1, shape[-1] // 4)) > 0.0625), 4, axis=-1).astype(np.float32)
    return mx_ref.flush(v.astype(BF))
C, T, M, R, G, O = 32, 256, 16, 3, 4, 2
def big(v):
    v = v.astype(np.float32)
    return np.where(np.abs(v) < np.float32(2.0 ** -16), np.float32(0), v).astype(BF)
def signed(rng, *shape):
    return (1 + rng.random(shape)) * rng.choice([-1.0, 1.0], shape)
def tiles(v):
    return np.ascontiguousarray(v.reshape(N, 128, -1).astype(np.float32).astype(BF))
def setup_inputs(rng):
    return {"c": big(f(rng, N, 128, 4 * C)), "x": big(f(rng, N, 128, 4 * T)), "u": f(rng, N, 128, 16), "w": f(rng, N, 128, 512 * O)}
def setup_inputs_dark(rng):
    d = setup_inputs(rng)
    top = np.arange(128) < 64
    kind = np.stack([rng.permutation(T) for r in range(N)]) < 2 * T // 3
    on = kind[:, None, :] == top[None, :, None]
    d["x"] = tiles((1.75 + 0.25 * rng.random((N, 128, T, 4))) * on[:, :, :, None] * 2.0 ** 29)
    d["u"] = tiles((2 + 0.2 * rng.random((N, 128, 4, 4))) * 2.0 ** 28)
    c = 0.5 * signed(rng, N * C, 128, 4)
    b = M + rng.permutation(N * C - M)[:2 * M]
    for half, e in ((top, b[:M + M // 2]), (~top, b[M + M // 2:])):
        c[np.ix_(e, np.flatnonzero(half))] = 2.5 + 0.5 * rng.random((len(e), 64, 4))
    d["c"] = tiles(c.reshape(N, C, 128, 4).transpose(0, 2, 1, 3) * 2.0 ** 28)
    return d
def setup_inputs_low(rng):
    d = setup_inputs(rng)
    s = np.where(np.stack([rng.permutation(T) for r in range(N)]) < 3 * T // 4, 1.0, -1.0)
    d["x"] = tiles(np.exp2(2 * rng.random((N, 128, T, 4))) * s[:, None, :, None] * 2.0 ** 28)
    d["u"] = tiles((1.85 + 2 * rng.random((N, 128, 4, 4))) * 2.0 ** 28)
    d["c"] = tiles((1.9 + 2 * rng.random((N, 128, C, 4)) + 0.1 * rng.random((N, 1, C, 1))) * 2.0 ** 28)
    return d
def setup_inputs_near(rng):
    d = setup_inputs(rng)
    c, x, u = np.zeros((N, 128, C, 4)), np.zeros((N, 128, T, 4)), np.zeros((N, 128, 4, 4))
    same = signed(rng, 64, 4)
    c[:, :64] = signed(rng, N, 64, C, 4)
    c[:, 80:88] = signed(rng, N, 8, C, 4) * 2.0 ** -3
    c[:, 112, :, 0] = 40
    c[:, 120, :, 0] = 0.25
    a, e = int(rng.integers(0, N)), rng.permutation(C)[:M]
    c[a][:64, e] = same[:, None, :]
    u[:, :64, 0] = same
    u[:, 112, 0, 0] = 40
    for r in range(N):
        h = rng.permutation(T) // 4
        i = np.zeros(T)
        i[np.argsort(h, kind="stable")] = np.arange(T) % 4 == 3
        x[r, :64] = signed(rng, 64, T // 4, 4)[:, h]
        x[r, 64:72] = signed(rng, 8, T, 4) * 2.0 ** -11
        x[r, 112, :, 0] = 40
        x[r, 120, :, 0] = (1 + i) * 2.0 ** -11
    d["c"], d["x"], d["u"] = tiles(c * 2.0 ** -4), tiles(x * 2.0 ** -4), tiles(u * 2.0 ** -4)
    return d
def setup_inputs_ties(rng):
    d = setup_inputs(rng)
    c, x, u = np.zeros((N, 128, C, 4)), np.zeros((N, 128, T, 4)), np.zeros((N, 128, 4, 4))
    h = rng.permutation(N * C) // (M // 2 + 3)
    p = signed(rng, 64, int(h.max()) + 1, 4)
    u[:, :64, 0] = p[:, 0]
    for r in range(N):
        c[r, :64] = p[:, h[C * r:C * r + C]]
        g = rng.permutation(T) // 4
        x[r, :64] = signed(rng, 64, T // 4, 4)[:, g]
        x[r, 64:] = signed(rng, 64, T, 4)
    d["c"], d["x"], d["u"] = tiles(c), tiles(x), tiles(u)
    return d
def setup_inputs_spread(rng):
    return {"c": big(wide(rng, N, 128, 4 * C, cols=6)), "x": big(wide(rng, N, 128, 4 * T, cols=6)), "u": wide(rng, N, 128, 16), "w": wide(rng, N, 128, 512 * O)}
def check_inputs(d):
    b = []
    for k, low in (("c", -16), ("x", -16), ("u", -30), ("w", -30)):
        v = np.abs(d[k].astype(np.float32))
        if not (np.isfinite(v).all() and ((v == 0) | (v >= 2.0 ** low) & (v <= 2.0 ** 30)).all()): b.append("a value of " + k)
    return b
def reference(c, x, u, w):
    every = join(*[mx_ref.quantize(np.ascontiguousarray(c[q])) for q in range(N)])
    tok = [mx_ref.quantize(np.ascontiguousarray(x[r])) for r in range(N)]
    s, mark = [], []
    for r in range(N):
        s.append(np.concatenate([mx_ref.matmul(pick(every, np.arange(i, i + 128)), tok[r]) for i in range(0, N * C, 128)]) + np.float32(0))
        a = np.concatenate([u[r], np.zeros((128, 496), BF)], axis=1)
        mark.append(mx_ref.matmul(mx_ref.quantize(a), tok[r])[0] + np.float32(0))
    free, won, made = np.ones(N * C, bool), [], []
    for t in range(R):
        gain = np.zeros(N * C, int)
        for r in range(N): gain = gain + np.sum(s[r] > mark[r], axis=1)
        win = np.argsort(np.where(free, -gain, 1), kind="stable")[:M]
        free[win] = False
        named = [np.argmax(s[r][win] - mark[r], axis=1) for r in range(N)]
        v = decode(pick(every, win))
        for i in range(G):
            v = (v + decode(join(*[pick(tok[(k + i) % N], named[(k + i) % N][k:k + 1]) for k in range(M)]))) * np.float32(0.5)
        q = mx_ref.quantize(np.ascontiguousarray(v.astype(BF)))
        full = pick(q, np.concatenate([np.arange(M), np.full(128 - M, -1)]))
        for r in range(N):
            z = mx_ref.matmul(full, tok[r])[:M] + np.float32(0)
            mark[r] = np.maximum(mark[r], np.max(z, axis=0))
        won.append(win)
        made.append(q)
    q = join(*made)
    n = R * M
    y, oc, osc = np.zeros((N, 128, O * n), np.float32), np.zeros((N, 128, 4 * n), np.uint8), np.zeros((N, 16, n), np.uint8)
    sel, mk = np.zeros((N, 1, n), np.float32), np.zeros((N, 1, T), np.float32)
    for r in range(N):
        for o in range(O): y[r, :, o * n:o * n + n] = mx_ref.matmul(mx_ref.quantize(np.ascontiguousarray(cut(w[r], o))), q)
        oc[r], osc[r] = emit(q)
        sel[r, 0] = np.concatenate(won)
        mk[r, 0] = mark[r]
    return {"y": y, "oc": oc, "osc": osc, "sel": sel, "mk": mk}

@@ -1,0 +1,430 @@
+from concourse.bass import DstId, RemoteDMATransfer
+from concourse.mybir import dt, AluOpType as ALU, AxisListType, ActivationFunctionType as AF
+
+M, R, O = 16, 3, 2
+BFT, F32, I32, U16, COD, PLN = "bfloat16", "float32", "int32", "uint16", "float8_e4m3fn_x4", "uint8"
+
+SCRATCH = {}
+
+
+def _sb(name, n, d):
+    SCRATCH[name] = ("sbuf", [128, n], d)
+
+
+def _codes(name, n):
+    _sb(name + "q", n, COD)
+    _sb(name + "s", n, PLN)
+
+
+for _n, _w in (("ctile", 512), ("zt", 512), ("xt", 1024), ("xu", 1024), ("wt", 1024), ("h", 512), ("ind", 512), ("ct", 512),
+               ("kt", 1024), ("oh", 512), ("ohn", 512), ("nm", 520), ("eb", 2048), ("ep", 1024), ("cm", 512), ("wgt", 512),
+               ("ones", 256), ("ident", 128), ("id256", 128), ("place", 128), ("placen", 16),
+               ("junk0", 256), ("junk1", 256), ("junk2", 256), ("junk3", 256)):
+    _sb(_n, _w, BFT)
+for _n, _w in (("mrow", 256), ("d0", 256), ("d1", 256), ("run0", 256), ("run1", 256), ("kcol", 2), ("ex", 2), ("fac", 80),
+               ("vrow", 80), ("vblk", 160), ("vtr", 160), ("yt", 96), ("selrow", 48), ("name", 2), ("won", 2)):
+    _sb(_n, _w, F32)
+for _b in range(4):
+    _sb("rec%d" % _b, 80, F32)
+for _t in range(R):
+    _sb("rk%d" % _t, 2, F32)
+for _t in range(R + 1):
+    _sb("mk%d" % _t, 64, F32)
+    _sb("mt%d" % _t, 64, F32)
+for _n, _w in (("pn", 2), ("pl", 2), ("ph", 2), ("vi", 80), ("vi2", 80)):
+    _sb(_n, _w, I32)
+_sb("offv", 6, U16)
+for _t in range(R):
+    _sb("off%d" % _t, 4, U16)
+    _codes("arr%d" % _t, 144)
+    _codes("win%d" % _t, 144)
+for _n, _w in (("c", 128), ("call", 256), ("x", 256), ("xu", 256), ("w", 256), ("v", 128), ("ind", 128), ("kt", 256),
+               ("oh", 128), ("ohn", 128), ("nm", 130), ("eb", 512), ("ep", 256), ("cm", 128), ("wgt", 128), ("vin", 128)):
+    _codes(_n, _w)
+for _b in range(8):
+    SCRATCH["ps%d" % _b] = ("psum", [128, 512], F32)
+
+SEMAPHORES = ["rc"] + ["rn%d" % t for t in range(R)] + ["rt%d" % t for t in range(R)] + ["ls"] + ["e%d" % i for i in range(120)]
+
+
+def _add(P, q, name, fn, r=(), w=(), inc=1, ext=None):
+    ops, tags = P["ops"], P["tags"]
+    i = len(ops)
+    deps = set()
+    if q == "G" and name[:3] != "snd":
+        w = list(w) + ["pool"]
+    for t in r:
+        s = tags.setdefault(t, {"w": None, "r": []})
+        if s["w"] is not None:
+            deps.add(s["w"])
+        if t[0] == "B":
+            deps.update(j for j in s["r"] if ops[j]["q"] != q)
+    for t in w:
+        s = tags.setdefault(t, {"w": None, "r": []})
+        if s["w"] is not None:
+            deps.add(s["w"])
+        deps.update(s["r"])
+    for t in r:
+        tags[t]["r"].append(i)
+    for t in w:
+        tags[t]["w"] = i
+        tags[t]["r"] = []
+    deps.discard(i)
+    ops.append({"q": q, "name": name, "fn": fn, "deps": deps, "inc": inc, "ext": ext})
+
+
+def _emit(P, g, T):
+    queues = {"G": g, "V": g.vector, "A": g.scalar, "P": g.tensor, "S": g.sync}
+    ops = P["ops"]
+    known = {q: 0 for q in queues}
+    done, waits, used = [], [], set()
+    for i, o in enumerate(ops):
+        if o["ext"] is not None:
+            done.append(1 << i)
+            waits.append([])
+            continue
+        need = []
+        for j in sorted(o["deps"], reverse=True):
+            if not known[o["q"]] >> j & 1:
+                need.append(j)
+                known[o["q"]] |= done[j]
+        keep = [j for j in need if not any(done[m] >> j & 1 for m in need if m != j)]
+        waits.append(sorted(keep))
+        used.update(keep)
+        done.append(known[o["q"]] | 1 << i)
+    pool, val = [], {}
+    for i, o in enumerate(ops):
+        if o["ext"] is not None:
+            val[i] = o["ext"]
+            continue
+        q = queues[o["q"]]
+        for j in waits[i]:
+            q.wait_ge(*val[j])
+        if o["fn"] is None:
+            continue
+        ins = o["fn"](q)
+        if i in used:
+            dma = o["inc"] > 1
+            free = [s for s in pool if not dma and not s["dma"] and done[i] >> s["last"] & 1]
+            free.sort(key=lambda s: -s["last"])
+            if free:
+                s = free[0]
+            else:
+                s = {"sem": T.sem["e%d" % len(pool)], "n": 0, "dma": dma}
+                pool.append(s)
+            s["last"] = i
+            s["n"] += o["inc"]
+            ins.then_inc(s["sem"], o["inc"])
+            val[i] = (s["sem"], s["n"])
+
+
+def rank_program(g, core, T, topo):
+    r = T.rank_of(core)
+    if r is None:
+        return
+    cores = list(T.cores)
+    N = len(cores)
+    P = {"ops": [], "tags": {}}
+    others = [q for q in range(N) if q != r]
+    mask = 0xFFFF
+    for q in others:
+        mask &= topo.mask(core, cores[q])
+    lanes = len([e for e in topo.engines(core, cores[others[0]]) if mask >> e & 1])
+    sent = [0]
+
+    def op(*a, **k):
+        _add(P, *a, **k)
+
+    def u8(ap):
+        return ap.bitcast(dt.uint8)
+
+    def w32(ap):
+        return ap.bitcast(dt.uint32)
+
+    def slot(src, dst):
+        return (src - dst) % N
+
+    def send(name, reads, src, dst, sem):
+        ids = []
+        for q in others:
+            rid, pid, _ = topo.addr(cores[q])
+            ids.append(DstId(rid=rid, pnc=pid))
+        dsts = [dst(q) for q in others]
+        sent[0] += lanes
+        op("G", name, lambda e: e.remote_dma_fused([RemoteDMATransfer(dst_ids=ids, dma_engine_mask=mask, remote_sem=T.sem[sem],
+                                                                      srcs=[src], dsts=dsts)], local_sem=T.sem.ls), r=reads)
+
+    def memset(name, ap, v, w):
+        op("V", name, lambda e: e.memset(ap, v), w=w)
+
+    def quant(name, out, c0, tile, a, n, r, w):
+        op("V", name, lambda e: e.quantize_mx(T[out + "q"][:, c0:c0 + n], T[out + "s"][:, c0:c0 + n], T[tile][:, a:a + 4 * n]), r=r, w=w)
+
+    def mm(name, bank, st, a, mv, b, n, r, start=True, stop=True):
+        op("P", name, lambda e: e.matmul_mx(T["ps%d" % bank][:, 0:n], T[st + "q"][:, a:a + 128], T[st + "s"][:, a:a + 128],
+                                            T[mv + "q"][:, b:b + n], T[mv + "s"][:, b:b + n], start, stop), r=r, w=["B%d" % bank])
+
+    def ps(bank, a, b):
+        return T["ps%d" % bank][:, a:b]
+
+    def ts(name, out, in0, s1, s2, o0, o1, r, w):
+        if o1 is None:
+            op("V", name, lambda e: e.tensor_scalar(out, in0, s1, None, o0), r=r, w=w)
+        else:
+            op("V", name, lambda e: e.tensor_scalar(out, in0, s1, s2, o0, o1), r=r, w=w)
+
+    def vcopy(name, out, in_, r, w):
+        op("V", name, lambda e: e.tensor_copy(out, in_), r=r, w=w)
+
+    def acopy(name, out, in_, r, w, **k):
+        op("A", name, lambda e: e.activation(out, in_, AF.Copy, **k), r=r, w=w)
+
+    def load(q, name, out, in_, r=(), w=()):
+        op(q, name, lambda e: e.dma_start(out, in_), r=r, w=w, inc=16)
+
+    order = [None] * M
+    for k in range(M):
+        i, h = (r - k) % N, k // N
+        order[(i % 4) + 4 * h + 8 * (i // 4)] = k
+    place_of = {k: j for j, k in enumerate(order)}
+    HT = ["h0", "h1", "h2", "h3"]
+    RND = 1.5 * 2.0 ** 27
+
+    load("S", "ldc", T.ctile[:, 0:128], T.c[:, :], w=["ctile"])
+    load("A", "ldx", T.xt[:, :], T.x[:, :], w=["xt"])
+    memset("ms_h", T.h[:], 0.0, HT + ["hu"])
+    load("S", "ldu", T.h[:, 60:64], T.u[:, 0:4], w=["hu"])
+    load("S", "ldw", T.wt[:, :], T.w[:, :], w=["wt"])
+    memset("ms_c", T.ctile[:, 128:512], 0.0, ["ctile0"])
+    memset("ms_ones", T.ones[:], 1.0, ["ones"])
+    memset("ms_zt", T.zt[:], 0.0, ["zt"])
+    for t in range(R):
+        quant("qz", "arr%d" % t, 0, "zt", 0, 128, ["zt"], ["arr%d" % t, "arrown%d" % t])
+    quant("qzv", "vin", 0, "zt", 0, 128, ["zt"], ["vin.q", "vin.s"])
+    memset("ms_ep", T.ep[:], 0.0, ["ep", "ep0", "ep1"])
+    op("G", "ident", lambda e: e.affine_select(T.ident[:], T.ones[:, 0:128], [[-1, 128]], ALU.is_equal, 0.0, 0, 1), r=["ones"], w=["ident"])
+    op("G", "ep0", lambda e: e.affine_select(T.ep[:, 0:1024:4], T.ones[:], [[1, 256]], ALU.is_equal, 0.0, 0, -2), r=["ones", "ep"], w=["ep0"])
+    memset("ms_ct", T.ct[:], 0.0, ["ct", "ct0", "ct1"])
+
+    quant("qc", "c", 0, "ctile", 0, 128, ["ctile", "ctile0"], ["c"])
+    send("snd_cq", ["c"] + ["arr%d" % t for t in range(R)], u8(T.cq[:, 0:32]), lambda q: u8(T.callq[:, 32 * r:32 * r + 32]), "rc")
+    send("snd_cs", ["c"], T.cs[:, 0:32], lambda q: T.calls[:, 32 * r:32 * r + 32], "rc")
+    load("S", "ownq", u8(T.callq[:, 32 * r:32 * r + 32]), u8(T.cq[:, 0:32]), r=["c"], w=["own.q"])
+    load("S", "owns", T.calls[:, 32 * r:32 * r + 32], T.cs[:, 0:32], r=["c"], w=["own.s"])
+    op("X", "arr_c", None, w=["call"], ext=(T.sem.rc, 2 * lanes * (N - 1)))
+    CALL = ["call", "own.q", "own.s"]
+
+    memset("ms_kt", T.kt[:], 0.0, ["kta", "ktb", "ktexa", "ktexb", "ktc", "ktd"])
+    quant("qx", "x", 0, "xt", 0, 256, ["xt"], ["x"])
+    for a in range(4):
+        for b in range(2):
+            acopy("xu%d%d" % (a, b), T.xu[:, 512 * b + 128 * a:512 * b + 128 * a + 128], T.xt[:, 256 * a + 128 * b:256 * a + 128 * b + 128],
+                  ["xt"], ["xu%d%d" % (a, b)])
+    quant("qv", "v", 0, "h", 0, 128, HT + ["hu"], ["v"])
+    quant("qxu", "xu", 0, "xu", 0, 256, ["xu%d%d" % (a, b) for a in range(4) for b in range(2)], ["xuq"])
+    for t in range(R + 1):
+        memset("ms_mk%d" % t, T["mk%d" % t][:], 0.0, ["mk%d.0" % t, "mk%d.1" % t])
+
+    def zmul():
+        for b in range(2):
+            mm("z%d" % b, 4 + b, "xu", 128 * b, "v", 0, 128, ["xuq", "v"])
+
+    def marks(t, b):
+        op("V", "mark%d" % b, lambda e: e.tensor_reduce(T["mk%d" % t][:, 32 * b:32 * b + 1], ps(4 + b, 15, 16 + M * t), AxisListType.X, ALU.max),
+           r=["B%d" % (4 + b)], w=["mk%d.%d" % (t, b)])
+
+    def turn(t):
+        op("V", "turn", lambda e: e.transpose(T["mt%d" % t][:], T["mk%d" % t][:]), r=["mk%d.0" % t, "mk%d.1" % t], w=["mt%d" % t])
+
+    def spread(t, aa):
+        for a in aa:
+            op("G", "spread%d" % a, lambda e, a=a: e.partition_broadcast(T.mrow[:, 64 * a:64 * a + 64], T["mt%d" % t][32 * a:32 * a + 1, :], 128),
+               r=["mt%d" % t], w=["mrow%d" % a])
+
+    zmul()
+    memset("ms_cm", T.cm[:], 0.0, ["cm"])
+    memset("ms_cm1", T.cm[:, 0:2], 1.0, ["cm"])
+    memset("ms_cm2", T.cm[:, 6:8], 1.0, ["cm"])
+    marks(0, 0)
+    marks(0, 1)
+    turn(0)
+    quant("qcm", "cm", 0, "cm", 0, 128, ["cm"], ["cmq"])
+    op("G", "ep1", lambda e: e.affine_select(T.ep[:, 1:1024:4], T.ones[:], [[1, 256]], ALU.is_equal, 0.0, -1, -2), r=["ones", "ep"], w=["ep1"])
+    op("G", "pn", lambda e: e.iota(T.pn[:], [[128, 2]], 0, 1), w=["pn"])
+    op("G", "vi", lambda e: e.iota(T.vi[:], [[4, 2], [16, 8], [17, 5]], 256 - 17 - 16 * r, 0), w=["vi"])
+    op("G", "placen", lambda e: e.iota(T.placen[:], [[-2, 16]], 255, 0, allow_small_or_imprecise_dtypes=True), w=["placen"])
+    op("G", "ktc", lambda e: e.iota(T.kt[32:33, 2:1024:4], [[0, 16], [-1, 16]], 15, 0, allow_small_or_imprecise_dtypes=True), w=["ktc"])
+    op("G", "ktd", lambda e: e.iota(T.kt[64:65, 2:1024:4], [[-16, 16], [0, 16]], 240, 0, allow_small_or_imprecise_dtypes=True), w=["ktd"])
+    spread(0, range(4))
+    for e_, v in enumerate((256.0, -4096.0, 1.0, 0.0)):
+        memset("ms_wgt", T.wgt[:, e_:512:4], v, ["wgt%d" % e_])
+    quant("qwgt", "wgt", 0, "wgt", 0, 128, ["wgt%d" % e_ for e_ in range(4)], ["wgtq"])
+    quant("qep", "ep", 0, "ep", 0, 256, ["ep0", "ep1", "ep"], ["epq"])
+    memset("ms_nm", T.nm[:], 0.0, ["nm", "nmlo", "nmhi"])
+    ts("pl", T.pl[:], T.pn[:], 15, None, ALU.bitwise_and, None, ["pn"], ["pl"])
+    ts("ph", T.ph[:], T.pn[:], 240, None, ALU.bitwise_and, None, ["pn"], ["ph"])
+    memset("ms_ex", T.ex[:], 0.0, ["ex"])
+    for j in range(M):
+        memset("place", T.place[:, j:128:16], 255.0 - 2.0 * order[j], ["place%d" % j])
+    vcopy("nm_l", T.nm[:, 0:2], T.pl[:], ["pl", "nm"], ["nm_l"])
+    vcopy("nm_h", T.nm[:, 8:10], T.ph[:], ["ph", "nm"], ["nm_h"])
+    memset("ms_oh", T.oh[:], 0.0, ["oh0", "oh1"])
+    ts("id256", T.id256[:], T.ident[:], 256.0, None, ALU.mult, None, ["ident"], ["id256"])
+
+    def eb_fill():
+        memset("ms_eb", T.eb[:], 0.0, ["eb0", "eb1", "eb2", "eb3"])
+        for b in range(4):
+            acopy("eb%d" % b, T.eb[:, 512 * b + b:512 * b + 512:4], T.ident[:], ["ident"], ["eb%d" % b])
+        memset("ms_fac", T.fac[:], 0.5, ["fac"])
+        memset("ms_fac0", T.fac[:, 0:80:5], 0.0, ["fac"])
+        memset("ms_fac1", T.fac[:, 1:80:5], 1.0, ["fac"])
+
+    def vlist():
+        ts("vi2", T.vi2[:], T.vi[:], 127, None, ALU.bitwise_and, None, ["vi"], ["vi2"])
+        vcopy("vrow", T.vrow[:], T.vi2[:], ["vi2"], ["vrow"])
+        for k in range(M):
+            op("V", "vrowk", lambda e, k=k: e.memset(T.vrow[:, 5 * k:5 * k + 1], float(128 + place_of[k])), r=["vrow"], w=["vrow.%d" % k])
+        for c in range(5):
+            for b in range(2):
+                acopy("vblk", T.vblk[:, 32 * c + 16 * b:32 * c + 16 * b + 16], T.vrow[:, 16 * c:16 * c + 16],
+                      ["vrow"] + ["vrow.%d" % k for k in range(M)], ["vblk%d%d" % (c, b)])
+        quant("qeb", "eb", 0, "eb", 0, 512, ["eb0", "eb1", "eb2", "eb3"], ["ebq"])
+        op("V", "vtr", lambda e: e.transpose(T.vtr[:], T.vblk[:]), r=["vblk%d%d" % (c, b) for c in range(5) for b in range(2)], w=["vtr"])
+        vcopy("offv", T.offv[:, 0:5], T.vtr[:, 0:160:32], ["vtr"], ["offv"])
+
+    def above(t, b):
+        ts("above%d" % b, T.ind[:, b:512:2], ps(b, 0, 256), T["mk%d" % t][:, 32 * b:32 * b + 1], None, ALU.is_gt, None,
+           ["B%d" % b, "mk%d.%d" % (t, b)], ["ind%d" % b])
+
+    def name_diff(b):
+        op("V", "diff%d" % b, lambda e: e.tensor_tensor(T["d%d" % b][:], ps(2 + b, 0, 256), T.mrow[:], ALU.subtract),
+           r=["B%d" % (2 + b)] + ["mrow%d" % a for a in range(4)], w=["d%d" % b])
+
+    def name_run(b):
+        op("V", "run%d" % b, lambda e: e.tensor_tensor_scan(T["run%d" % b][:], T["d%d" % b][:], T["d%d" % b][:], -1e29, ALU.max, ALU.max),
+           r=["d%d" % b], w=["run%d" % b])
+
+    def name_at(b):
+        op("A", "name%d" % b, lambda e: e.activation(T["junk%d" % b][:], T["run%d" % b][:], AF.Sign, bias=T["run%d" % b][:, 255:256], scale=-1.0,
+                                                     accum_out=T.name[:, b:b + 1]), r=["run%d" % b], w=["junk%d" % b, "name%d" % b])
+
+    def one_round(t):
+        arr, win, off, rk = "arr%d" % t, "win%d" % t, "off%d" % t, "rk%d" % t
+        if t == 0:
+            for b in range(2):
+                mm("sb%d" % b, b, "xu", 128 * b, "call", 0, 256, ["xuq"] + CALL)
+        else:
+            marks(t, 0)
+            marks(t, 1)
+        above(t, 0)
+        if t:
+            turn(t)
+        above(t, 1)
+        quant("qind", "ind", 0, "ind", 0, 128, ["ind0", "ind1"], ["indq"])
+        if t:
+            spread(t, (0, 1))
+        mm("cnt", 6, "ind", 0, "cm", 0, 128, ["indq", "cmq"])
+        ts("c16", T.ct[:, 0:2], ps(6, 0, 2), RND, RND, ALU.add, ALU.subtract, ["B6", "ct"], ["ct0"])
+        op("V", "crest", lambda e: e.tensor_tensor(T.ct[:, 4:6], ps(6, 0, 2), T.ct[:, 0:2], ALU.subtract), r=["B6", "ct0", "ct"], w=["ct1"])
+        quant("qct", arr, 16, "ct", 0, 128, ["ct", "ct0", "ct1"], ["arrown%d" % t])
+        send("snd_nq", ["arrown%d" % t], u8(T[arr + "q"][:, 16:18]),
+             lambda q: u8(T[arr + "q"][:, 2 * slot(r, q) - 2:2 * slot(r, q)]), "rn%d" % t)
+        send("snd_ns", ["arrown%d" % t], T[arr + "s"][:, 16:18],
+             lambda q: T[arr + "s"][:, 2 * slot(r, q) - 2:2 * slot(r, q)], "rn%d" % t)
+        op("X", "arr_n", None, w=["land" + arr], ext=(T.sem["rn%d" % t], 2 * lanes * (N - 1)))
+        if t:
+            spread(t, (2, 3))
+        else:
+            for b in range(2):
+                mm("sa%d" % b, 2 + b, "call", 128 * b, "x", 0, 256, ["x"] + CALL)
+        name_diff(0)
+        name_diff(1)
+        name_run(0)
+        name_at(0)
+        name_run(1)
+        name_at(1)
+        if t == 0:
+            eb_fill()
+        if t == 1:
+            quant("qw", "w", 0, "wt", 0, 256, ["wt"], ["w"])
+            memset("ms_ohn", T.ohn[:], 0.0, ["ohn"])
+        for b in range(2):
+            mm("gain%d" % b, 4 + b, arr, 0, "ep", 128 * b, 128, ["land" + arr, "arr%d" % t, "arrown%d" % t, "epq"])
+        vcopy("gcopy0", T.kt[:, 0:512:4], ps(4, 0, 128), ["B4"], ["kta"])
+        acopy("gcopy1", T.kt[:, 512:1024:4], ps(5, 0, 128), ["B5"], ["ktb"])
+        quant("qkta", "kt", 0, "kt", 0, 128, ["kta", "ktexa", "ktc", "ktd"], ["ktqa"])
+        quant("qktb", "kt", 128, "kt", 512, 128, ["ktb", "ktexb", "ktc", "ktd"], ["ktqb"])
+        mm("kcol0", 6, "kt", 0, "wgt", 0, 128, ["ktqa", "wgtq"])
+        mm("krow", 7, "wgt", 0, "kt", 0, 256, ["ktqa", "ktqb", "wgtq"])
+        mm("kcol1", 4, "kt", 128, "wgt", 0, 128, ["ktqb", "wgtq"])
+        vcopy("kcc0", T.kcol[:, 0:1], ps(6, 0, 1), ["B6"], ["kcol0"])
+        ts("n16", T.nm[:, 24:26], T.name[:], RND, RND, ALU.add, ALU.subtract, ["name0", "name1", "nm"], ["nmhi"])
+        vcopy("kcc1", T.kcol[:, 1:2], ps(4, 0, 1), ["B4"], ["kcol1"])
+        op("V", "nrest", lambda e: e.tensor_tensor(T.nm[:, 16:18], T.name[:], T.nm[:, 24:26], ALU.subtract), r=["name0", "name1", "nmhi", "nm"], w=["nmlo"])
+        quant("qnm", "nm", 0, "nm", 0, 130, ["nm", "nm_l", "nm_h", "nmlo", "nmhi"], ["nmq"])
+        for b in range(2):
+            op("A", "rank%d" % b, lambda e, b=b: e.activation(T["junk%d" % (2 + b)][:], ps(7, 0, 256), AF.Sign, bias=T.kcol[:, b:b + 1], scale=-1.0,
+                                                              accum_out=T[rk][:, b:b + 1]), r=["B7", "kcol%d" % b], w=["junk%d" % (2 + b), "%s.%d" % (rk, b)])
+        PL = ["place%d" % j for j in range(M)]
+        for b in range(2):
+            ts("onehot%d" % b, T.oh[:, b:512:4], T.place[:], T[rk][:, b:b + 1], None, ALU.is_equal, None, ["%s.%d" % (rk, b)] + PL, ["oh%d" % b])
+        quant("qoh", "oh", 0, "oh", 0, 128, ["oh0", "oh1"], ["ohq"])
+        mm("lists", 5, "oh", 0, "nm", 0, 128, ["ohq", "nmq"])
+        ts("offt", T[off][:, 0:1], ps(5, 4, 5), ps(5, 6, 7), None, ALU.add, None, ["B5"], [off + "t"])
+        op("V", "tokq", lambda e: e.tensor_copy(w32(T[win + "q"][:, 0:16]), w32(T.xq[:, 0:256]).indirect(T[off][:, 0:1])), r=["x", off + "t"], w=[win + ".tq"])
+        op("A", "toks", lambda e: e.activation(T[win + "s"][:, 0:16], T.xs[:, 0:256].indirect(T[off][:, 0:1]), AF.Copy), r=["x", off + "t"], w=[win + ".ts"])
+        send("snd_tq", [win + ".tq"], u8(T[win + "q"][:, 0:8]), lambda q: u8(T[win + "q"][:, 16 * slot(r, q):16 * slot(r, q) + 8]), "rt%d" % t)
+        send("snd_ts", [win + ".ts"], T[win + "s"][:, 0:8], lambda q: T[win + "s"][:, 16 * slot(r, q):16 * slot(r, q) + 8], "rt%d" % t)
+        op("X", "arr_t", None, w=["land" + win], ext=(T.sem["rt%d" % t], 2 * lanes * (N - 1)))
+        ts("offc", T[off][:, 2:3], ps(5, 0, 1), ps(5, 2, 3), None, ALU.add, None, ["B5"], [off + "c"])
+        op("V", "candq", lambda e: e.tensor_copy(w32(T[win + "q"][:, 128:144]), w32(T.callq[:, 0:256]).indirect(T[off][:, 2:3])), r=CALL + [off + "c"], w=[win + ".cq"])
+        op("A", "cands", lambda e: e.activation(T[win + "s"][:, 128:144], T.calls[:, 0:256].indirect(T[off][:, 2:3]), AF.Copy), r=CALL + [off + "c"], w=[win + ".cs"])
+        if t + 1 < R:
+            ts("won", T.won[:], T[rk][:], 224.0, None, ALU.is_gt, None, [rk + ".0", rk + ".1"], ["won"])
+            op("V", "ex", lambda e: e.tensor_tensor(T.ex[:], T.ex[:], T.won[:], ALU.add), r=["won"], w=["ex"])
+            for b in range(2):
+                ts("ktex%d" % b, T.kt[:, 512 * b + 1:512 * b + 512:4], T.id256[:], T.ex[:, b:b + 1], None, ALU.mult, None, ["id256", "ex"], ["ktex" + "ab"[b]])
+        else:
+            for s in range(R):
+                for b in range(2):
+                    ts("ohn", T.ohn[:, 64 * s + b:64 * s + 64:4], T.placen[:], T["rk%d" % s][:, b:b + 1], None, ALU.is_equal, None,
+                       ["ohn", "placen", "rk%d.%d" % (s, b)], ["ohn%d%d" % (s, b)])
+            quant("qohn", "ohn", 0, "ohn", 0, 128, ["ohn"] + ["ohn%d%d" % (s, b) for s in range(R) for b in range(2)], ["ohnq"])
+            mm("sel0", 6, "nm", 0, "ohn", 0, 128, ["nmq", "ohnq"], True, False)
+            mm("sel1", 6, "nm", 2, "ohn", 0, 128, ["nmq", "ohnq"], False, True)
+            acopy("selrow", T.selrow[0:1, :], T.ps6[0:1, 0:48], ["B6"], ["selrow"])
+            load("S", "st_sel", T.sel[0:1, :], T.selrow[0:1, :], r=["selrow"], w=["out.sel"])
+        if t == 0:
+            vlist()
+        WIN = ["land" + win, win + ".tq", win + ".ts", win + ".cq", win + ".cs", "offv"]
+        op("V", "vinq", lambda e: e.tensor_copy(w32(T.vinq[:, 0:80]), w32(T[win + "q"][:, 0:144]).indirect(T.offv[:, 0:5])), r=WIN, w=["vin.q"])
+        op("A", "vins", lambda e: e.activation(T.vins[:, 0:80], T[win + "s"][:, 0:144].indirect(T.offv[:, 0:5]), AF.Copy), r=WIN, w=["vin.s"])
+        for b in range(4):
+            mm("dec%d" % b, 4 + b, "eb", 128 * b, "vin", 0, 128, ["ebq", "vin.q", "vin.s"])
+        for b in range(4):
+            op("V", "rec%d" % b, lambda e, b=b: e.tensor_tensor_scan(T["rec%d" % b][:], T.fac[:], ps(4 + b, 0, 80), 0.0, ALU.mult, ALU.add),
+               r=["B%d" % (4 + b), "fac"], w=["rec%d" % b])
+            acopy("cast%d" % b, T.h[:, 64 * (t + 1) + b:64 * (t + 2):4], T["rec%d" % b][:, 4:80:5], ["rec%d" % b], ["h%d" % b], scale=0.5)
+        quant("qv", "v", 0, "h", 0, 128, HT + ["hu"], ["v"])
+        zmul()
+
+    for t in range(R):
+        one_round(t)
+
+    n = R * M
+    load("S", "st_oc", T.oc[:, :], u8(T.vq[:, 16:16 + n]), r=["v"], w=["out.oc"])
+    for k in range(4):
+        load("A" if k % 2 else "S", "st_osc%d" % k, T.osc[4 * k:4 * k + 4, :], T.vs[32 * k:32 * k + 4, 16:16 + n], r=["v"], w=["out.osc%d" % k])
+    marks(R, 0)
+    marks(R, 1)
+    turn(R)
+    for o in range(O):
+        mm("y%d" % o, 6 + o, "w", 128 * o, "v", 0, 128, ["w", "v"])
+    acopy("yc0", T.yt[:, 0:n], ps(6, 16, 16 + n), ["B6"], ["yt0"])
+    vcopy("yc1", T.yt[:, n:2 * n], ps(7, 16, 16 + n), ["B7"], ["yt1"])
+    load("S", "st_y", T.y[:, :], T.yt[:], r=["yt0", "yt1"], w=["out.y"])
+    for a in range(4):
+        load("A" if a % 2 else "S", "st_mk%d" % a, T.mk[0:1, 64 * a:64 * a + 64], T["mt%d" % R][32 * a:32 * a + 1, :], r=["mt%d" % R], w=["out.mk%d" % a])
+    op("S", "end", None, r=["out.sel", "out.oc", "out.y"] + ["out.osc%d" % k for k in range(4)] + ["out.mk%d" % a for a in range(4)])
+    _emit(P, g, T)
+    g.wait_ge(T.sem.ls, sent[0])

@@ -16,35 +16,38 @@ def _codes(name, n):
     _sb(name + "s", n, PLN)
 
 
-for _n, _w in (("ctile", 512), ("zt", 512), ("xt", 1024), ("xu", 1024), ("wt", 1024), ("h", 512), ("ind", 512), ("ct", 512),
-               ("kt", 1024), ("oh", 512), ("ohn", 512), ("nm", 520), ("eb", 2048), ("ep", 1024), ("cm", 512), ("wgt", 512),
-               ("ones", 256), ("ident", 128), ("id256", 128), ("place", 128), ("placen", 16),
+for _n, _w in (("ctile", 512), ("zt", 512), ("xt", 1024), ("xu", 1024), ("wt", 1024), ("h", 512), ("ind", 512), ("tab", 2048),
+               ("kt", 1024), ("oh", 512), ("ohn", 512), ("nm", 520), ("eb", 2048), ("cm", 512), ("wgt", 512),
+               ("ones", 128), ("ident", 128), ("place", 128), ("placen", 16),
                ("junk0", 256), ("junk1", 256), ("junk2", 256), ("junk3", 256)):
     _sb(_n, _w, BFT)
-for _n, _w in (("mrow", 256), ("d0", 256), ("d1", 256), ("run0", 256), ("run1", 256), ("kcol", 2), ("ex", 2), ("fac", 80),
-               ("vrow", 80), ("vblk", 160), ("vtr", 160), ("yt", 96), ("selrow", 48), ("name", 2), ("won", 2)):
+for _n, _w in (("mrow", 256), ("d0", 256), ("d1", 256), ("run0", 256), ("run1", 256), ("kcol", 2), ("cap", 2), ("o16", 2),
+               ("tot", 2), ("gmask", 8), ("md", 3), ("step", 7), ("fac", 80), ("vrow", 80), ("vblk", 160), ("vtr", 160),
+               ("yt", 96), ("selrow", 48), ("name", 2), ("won", 2)):
     _sb(_n, _w, F32)
 for _b in range(4):
     _sb("rec%d" % _b, 80, F32)
 for _t in range(R):
-    _sb("rk%d" % _t, 2, F32)
+    _sb("rk%d" % _t, 4, F32)
 for _t in range(R + 1):
     _sb("mk%d" % _t, 64, F32)
     _sb("mt%d" % _t, 64, F32)
-for _n, _w in (("pn", 2), ("pl", 2), ("ph", 2), ("vi", 80), ("vi2", 80)):
+for _n, _w in (("pn", 2), ("pl", 2), ("ph", 2), ("vi", 80), ("vi2", 80), ("gm", 8), ("gm2", 8), ("v16", 16)):
     _sb(_n, _w, I32)
 _sb("offv", 6, U16)
+_sb("offk", 16, U16)
 for _t in range(R):
     _sb("off%d" % _t, 4, U16)
-    _codes("arr%d" % _t, 144)
+    _sb("cnt%d" % _t, 2, BFT)
+    _sb("land%d" % _t, 14, BFT)
     _codes("win%d" % _t, 144)
 for _n, _w in (("c", 128), ("call", 256), ("x", 256), ("xu", 256), ("w", 256), ("v", 128), ("ind", 128), ("kt", 256),
-               ("oh", 128), ("ohn", 128), ("nm", 130), ("eb", 512), ("ep", 256), ("cm", 128), ("wgt", 128), ("vin", 128)):
+               ("oh", 128), ("ohn", 128), ("nm", 130), ("eb", 512), ("cm", 128), ("wgt", 128), ("vin", 128)):
     _codes(_n, _w)
 for _b in range(8):
     SCRATCH["ps%d" % _b] = ("psum", [128, 512], F32)
 
-SEMAPHORES = ["rc"] + ["rn%d" % t for t in range(R)] + ["rt%d" % t for t in range(R)] + ["ls"] + ["e%d" % i for i in range(120)]
+SEMAPHORES = ["rc"] + ["rn%d" % t for t in range(R)] + ["rt%d" % t for t in range(R)] + ["ls"] + ["e%d" % i for i in range(140)]
 
 
 def _add(P, q, name, fn, r=(), w=(), inc=1, ext=None):
@@ -173,6 +176,9 @@ def rank_program(g, core, T, topo):
         else:
             op("V", name, lambda e: e.tensor_scalar(out, in0, s1, s2, o0, o1), r=r, w=w)
 
+    def tt(name, out, in0, in1, o, r, w):
+        op("V", name, lambda e: e.tensor_tensor(out, in0, in1, o), r=r, w=w)
+
     def vcopy(name, out, in_, r, w):
         op("V", name, lambda e: e.tensor_copy(out, in_), r=r, w=w)
 
@@ -188,42 +194,52 @@ def rank_program(g, core, T, topo):
         order[(i % 4) + 4 * h + 8 * (i // 4)] = k
     place_of = {k: j for j, k in enumerate(order)}
     HT = ["h0", "h1", "h2", "h3"]
+    EB = ["eb0", "eb1", "eb2", "eb3"]
     RND = 1.5 * 2.0 ** 27
 
     load("S", "ldc", T.ctile[:, 0:128], T.c[:, :], w=["ctile"])
     load("A", "ldx", T.xt[:, :], T.x[:, :], w=["xt"])
     memset("ms_h", T.h[:], 0.0, HT + ["hu"])
     load("S", "ldu", T.h[:, 60:64], T.u[:, 0:4], w=["hu"])
-    load("S", "ldw", T.wt[:, :], T.w[:, :], w=["wt"])
     memset("ms_c", T.ctile[:, 128:512], 0.0, ["ctile0"])
     memset("ms_ones", T.ones[:], 1.0, ["ones"])
     memset("ms_zt", T.zt[:], 0.0, ["zt"])
-    for t in range(R):
-        quant("qz", "arr%d" % t, 0, "zt", 0, 128, ["zt"], ["arr%d" % t, "arrown%d" % t])
     quant("qzv", "vin", 0, "zt", 0, 128, ["zt"], ["vin.q", "vin.s"])
-    memset("ms_ep", T.ep[:], 0.0, ["ep", "ep0", "ep1"])
-    op("G", "ident", lambda e: e.affine_select(T.ident[:], T.ones[:, 0:128], [[-1, 128]], ALU.is_equal, 0.0, 0, 1), r=["ones"], w=["ident"])
-    op("G", "ep0", lambda e: e.affine_select(T.ep[:, 0:1024:4], T.ones[:], [[1, 256]], ALU.is_equal, 0.0, 0, -2), r=["ones", "ep"], w=["ep0"])
-    memset("ms_ct", T.ct[:], 0.0, ["ct", "ct0", "ct1"])
+    memset("ms_cm", T.cm[:], 0.0, ["cm0", "cm1", "cm2"])
+    memset("ms_kt", T.kt[:], 0.0, ["kta", "ktb", "kto0", "kto1", "ktr0", "ktr1", "ktc", "ktd"])
+    memset("ms_cm1", T.cm[:, 0:2], 1.0, ["cm1"])
+    memset("ms_cm2", T.cm[:, 6:8], 1.0, ["cm2"])
+    op("G", "pn", lambda e: e.iota(T.pn[:], [[128, 2]], 0, 1), w=["pn"])
+    op("G", "vi", lambda e: e.iota(T.vi[:], [[4, 2], [16, 8], [17, 5]], 256 - 17 - 16 * r, 0), w=["vi"])
+    op("G", "v16", lambda e: e.iota(T.v16[:], [[1, 16]], 0, 0), w=["v16"])
+    op("G", "gm", lambda e: e.iota(T.gm[:], [[-16, 8]], 0, 1), w=["gm"])
+    op("G", "ident", lambda e: e.affine_select(T.ident[:], T.ones[:], [[-1, 128]], ALU.is_equal, 0.0, 0, 1), r=["ones"], w=["ident"])
 
     quant("qc", "c", 0, "ctile", 0, 128, ["ctile", "ctile0"], ["c"])
-    send("snd_cq", ["c"] + ["arr%d" % t for t in range(R)], u8(T.cq[:, 0:32]), lambda q: u8(T.callq[:, 32 * r:32 * r + 32]), "rc")
+    send("snd_cq", ["c"], u8(T.cq[:, 0:32]), lambda q: u8(T.callq[:, 32 * r:32 * r + 32]), "rc")
     send("snd_cs", ["c"], T.cs[:, 0:32], lambda q: T.calls[:, 32 * r:32 * r + 32], "rc")
     load("S", "ownq", u8(T.callq[:, 32 * r:32 * r + 32]), u8(T.cq[:, 0:32]), r=["c"], w=["own.q"])
     load("S", "owns", T.calls[:, 32 * r:32 * r + 32], T.cs[:, 0:32], r=["c"], w=["own.s"])
     op("X", "arr_c", None, w=["call"], ext=(T.sem.rc, 2 * lanes * (N - 1)))
     CALL = ["call", "own.q", "own.s"]
 
-    memset("ms_kt", T.kt[:], 0.0, ["kta", "ktb", "ktexa", "ktexb", "ktc", "ktd"])
-    quant("qx", "x", 0, "xt", 0, 256, ["xt"], ["x"])
+    for j in range(M):
+        acopy("place", T.place[:, j:128:16], T.ones[:, 0:8], ["ones"], ["place%d" % j], scale=255.0 - 2.0 * order[j])
+    acopy("z_nm", T.nm[:, 0:512], T.zt[:], ["zt"], ["nm", "nmlo", "nmhi"])
     for a in range(4):
         for b in range(2):
-            acopy("xu%d%d" % (a, b), T.xu[:, 512 * b + 128 * a:512 * b + 128 * a + 128], T.xt[:, 256 * a + 128 * b:256 * a + 128 * b + 128],
-                  ["xt"], ["xu%d%d" % (a, b)])
+            (vcopy if b else acopy)("xu", T.xu[:, 512 * b + 128 * a:512 * b + 128 * a + 128], T.xt[:, 256 * a + 128 * b:256 * a + 128 * b + 128],
+                                    ["xt"], ["xu%d%d" % (a, b)])
+    acopy("z_oh", T.oh[:], T.zt[:], ["zt"], ["oh0", "oh1"])
+    quant("qx", "x", 0, "xt", 0, 256, ["xt"], ["x"])
     quant("qv", "v", 0, "h", 0, 128, HT + ["hu"], ["v"])
-    quant("qxu", "xu", 0, "xu", 0, 256, ["xu%d%d" % (a, b) for a in range(4) for b in range(2)], ["xuq"])
+    memset("z_nm2", T.nm[:, 512:520], 0.0, ["nm2"])
     for t in range(R + 1):
         memset("ms_mk%d" % t, T["mk%d" % t][:], 0.0, ["mk%d.0" % t, "mk%d.1" % t])
+    quant("qxu", "xu", 0, "xu", 0, 256, ["xu%d%d" % (a, b) for a in range(4) for b in range(2)], ["xuq"])
+    quant("qcm", "cm", 0, "cm", 0, 128, ["cm0", "cm1", "cm2"], ["cmq"])
+    for e_, v in enumerate((256.0, 256.0, 1.0, 256.0)):
+        memset("ms_wgt", T.wgt[:, e_:512:4], v, ["wgt%d" % e_])
 
     def zmul():
         for b in range(2):
@@ -242,63 +258,49 @@ def rank_program(g, core, T, topo):
                r=["mt%d" % t], w=["mrow%d" % a])
 
     zmul()
-    memset("ms_cm", T.cm[:], 0.0, ["cm"])
-    memset("ms_cm1", T.cm[:, 0:2], 1.0, ["cm"])
-    memset("ms_cm2", T.cm[:, 6:8], 1.0, ["cm"])
+    ts("pl", T.pl[:], T.pn[:], 15, None, ALU.bitwise_and, None, ["pn"], ["pl"])
+    ts("vi2", T.vi2[:], T.vi[:], 127, None, ALU.bitwise_and, None, ["vi"], ["vi2"])
     marks(0, 0)
     marks(0, 1)
+    vcopy("vrow", T.vrow[:], T.vi2[:], ["vi2"], ["vrow"])
     turn(0)
-    quant("qcm", "cm", 0, "cm", 0, 128, ["cm"], ["cmq"])
-    op("G", "ep1", lambda e: e.affine_select(T.ep[:, 1:1024:4], T.ones[:], [[1, 256]], ALU.is_equal, 0.0, -1, -2), r=["ones", "ep"], w=["ep1"])
-    op("G", "pn", lambda e: e.iota(T.pn[:], [[128, 2]], 0, 1), w=["pn"])
-    op("G", "vi", lambda e: e.iota(T.vi[:], [[4, 2], [16, 8], [17, 5]], 256 - 17 - 16 * r, 0), w=["vi"])
-    op("G", "placen", lambda e: e.iota(T.placen[:], [[-2, 16]], 255, 0, allow_small_or_imprecise_dtypes=True), w=["placen"])
-    op("G", "ktc", lambda e: e.iota(T.kt[32:33, 2:1024:4], [[0, 16], [-1, 16]], 15, 0, allow_small_or_imprecise_dtypes=True), w=["ktc"])
-    op("G", "ktd", lambda e: e.iota(T.kt[64:65, 2:1024:4], [[-16, 16], [0, 16]], 240, 0, allow_small_or_imprecise_dtypes=True), w=["ktd"])
-    spread(0, range(4))
-    for e_, v in enumerate((256.0, -4096.0, 1.0, 0.0)):
-        memset("ms_wgt", T.wgt[:, e_:512:4], v, ["wgt%d" % e_])
     quant("qwgt", "wgt", 0, "wgt", 0, 128, ["wgt%d" % e_ for e_ in range(4)], ["wgtq"])
-    quant("qep", "ep", 0, "ep", 0, 256, ["ep0", "ep1", "ep"], ["epq"])
-    memset("ms_nm", T.nm[:], 0.0, ["nm", "nmlo", "nmhi"])
-    ts("pl", T.pl[:], T.pn[:], 15, None, ALU.bitwise_and, None, ["pn"], ["pl"])
+    op("G", "ktc", lambda e: e.iota(T.kt[32:33, 2:1024:4], [[0, 16], [-1, 16]], 15, 0, allow_small_or_imprecise_dtypes=True), w=["ktc", "ktc2"])
+    spread(0, (0, 1, 2))
+    for d in range(3):
+        ts("md", T.md[:, d:d + 1], T.pl[:, 0:1], 3.0 + d, None, ALU.is_equal, None, ["pl"], ["md%d" % d])
+    memset("ms_cap", T.cap[:], 256.0, ["cap"])
+    ts("tab", T.tab[:, 0:16], T.v16[:], T.md[:, 0:1], None, ALU.mult, None, ["v16", "md0"], ["tab0"])
+    for k in range(7):
+        ts("step", T.step[:, k:k + 1], T.md[:, 1 + k // 4:2 + k // 4], 16.0 * 2 ** k, None, ALU.mult, None, ["md%d" % (1 + k // 4)], ["step%d" % k])
+    for k in range(5):
+        m = 16 << k
+        ts("tab", T.tab[:, m:2 * m], T.tab[:, 0:m], T.step[:, k:k + 1], None, ALU.add, None, ["tab%d" % j for j in range(k + 1)] + ["step%d" % k], ["tab%d" % (k + 1)])
+    TAB = ["tab%d" % j for j in range(8)]
+    memset("kt32", T.kt[32:33, 130:1024:512], 0.0, ["ktc"])
+    memset("kt96", T.kt[96:97, 130:1024:512], 15.0, ["ktc2"])
+    ts("gm2", T.gm2[:], T.gm[:], 4, None, ALU.arith_shift_right, None, ["gm"], ["gm2"])
     ts("ph", T.ph[:], T.pn[:], 240, None, ALU.bitwise_and, None, ["pn"], ["ph"])
-    memset("ms_ex", T.ex[:], 0.0, ["ex"])
-    for j in range(M):
-        memset("place", T.place[:, j:128:16], 255.0 - 2.0 * order[j], ["place%d" % j])
     vcopy("nm_l", T.nm[:, 0:2], T.pl[:], ["pl", "nm"], ["nm_l"])
+    ts("gmask", T.gmask[:], T.gm2[:], 0.0, None, ALU.is_equal, None, ["gm2"], ["gmask"])
     vcopy("nm_h", T.nm[:, 8:10], T.ph[:], ["ph", "nm"], ["nm_h"])
-    memset("ms_oh", T.oh[:], 0.0, ["oh0", "oh1"])
-    ts("id256", T.id256[:], T.ident[:], 256.0, None, ALU.mult, None, ["ident"], ["id256"])
-
-    def eb_fill():
-        memset("ms_eb", T.eb[:], 0.0, ["eb0", "eb1", "eb2", "eb3"])
-        for b in range(4):
-            acopy("eb%d" % b, T.eb[:, 512 * b + b:512 * b + 512:4], T.ident[:], ["ident"], ["eb%d" % b])
-        memset("ms_fac", T.fac[:], 0.5, ["fac"])
-        memset("ms_fac0", T.fac[:, 0:80:5], 0.0, ["fac"])
-        memset("ms_fac1", T.fac[:, 1:80:5], 1.0, ["fac"])
-
-    def vlist():
-        ts("vi2", T.vi2[:], T.vi[:], 127, None, ALU.bitwise_and, None, ["vi"], ["vi2"])
-        vcopy("vrow", T.vrow[:], T.vi2[:], ["vi2"], ["vrow"])
-        for k in range(M):
-            op("V", "vrowk", lambda e, k=k: e.memset(T.vrow[:, 5 * k:5 * k + 1], float(128 + place_of[k])), r=["vrow"], w=["vrow.%d" % k])
-        for c in range(5):
-            for b in range(2):
-                acopy("vblk", T.vblk[:, 32 * c + 16 * b:32 * c + 16 * b + 16], T.vrow[:, 16 * c:16 * c + 16],
-                      ["vrow"] + ["vrow.%d" % k for k in range(M)], ["vblk%d%d" % (c, b)])
-        quant("qeb", "eb", 0, "eb", 0, 512, ["eb0", "eb1", "eb2", "eb3"], ["ebq"])
-        op("V", "vtr", lambda e: e.transpose(T.vtr[:], T.vblk[:]), r=["vblk%d%d" % (c, b) for c in range(5) for b in range(2)], w=["vtr"])
-        vcopy("offv", T.offv[:, 0:5], T.vtr[:, 0:160:32], ["vtr"], ["offv"])
+    for k in range(M):
+        acopy("vrowk", T.vrow[:, 5 * k:5 * k + 1], T.ones[:, 0:1], ["vrow", "ones"], ["vrow.%d" % k], scale=float(128 + place_of[k]))
+    for c in range(5):
+        for b in range(2):
+            acopy("vblk", T.vblk[:, 32 * c + 16 * b:32 * c + 16 * b + 16], T.vrow[:, 16 * c:16 * c + 16],
+                  ["vrow"] + ["vrow.%d" % k for k in range(M)], ["vblk%d%d" % (c, b)])
+    for k in (5, 6):
+        op("A", "tab", lambda e, m=16 << k, k=k: e.activation(T.tab[:, m:2 * m], T.tab[:, 0:m], AF.Identity, bias=T.step[:, k:k + 1]),
+           r=["tab%d" % j for j in range(k + 1)] + ["step%d" % k], w=["tab%d" % (k + 1)])
 
     def above(t, b):
-        ts("above%d" % b, T.ind[:, b:512:2], ps(b, 0, 256), T["mk%d" % t][:, 32 * b:32 * b + 1], None, ALU.is_gt, None,
-           ["B%d" % b, "mk%d.%d" % (t, b)], ["ind%d" % b])
+        for k in range(2):
+            ts("above", T.ind[:, 2 * k + b:512:4], ps(b, 128 * k, 128 * k + 128), T["mk%d" % t][:, 32 * b:32 * b + 1], None, ALU.is_gt, None,
+               ["B%d" % b, "mk%d.%d" % (t, b)], ["ind%d%d" % (b, k)])
 
     def name_diff(b):
-        op("V", "diff%d" % b, lambda e: e.tensor_tensor(T["d%d" % b][:], ps(2 + b, 0, 256), T.mrow[:], ALU.subtract),
-           r=["B%d" % (2 + b)] + ["mrow%d" % a for a in range(4)], w=["d%d" % b])
+        tt("diff%d" % b, T["d%d" % b][:], ps(2 + b, 0, 256), T.mrow[:], ALU.subtract, ["B%d" % (2 + b)] + ["mrow%d" % a for a in range(4)], ["d%d" % b])
 
     def name_run(b):
         op("V", "run%d" % b, lambda e: e.tensor_tensor_scan(T["run%d" % b][:], T["d%d" % b][:], T["d%d" % b][:], -1e29, ALU.max, ALU.max),
@@ -309,32 +311,34 @@ def rank_program(g, core, T, topo):
                                                      accum_out=T.name[:, b:b + 1]), r=["run%d" % b], w=["junk%d" % b, "name%d" % b])
 
     def one_round(t):
-        arr, win, off, rk = "arr%d" % t, "win%d" % t, "off%d" % t, "rk%d" % t
+        win, off, rk, cnt, land = "win%d" % t, "off%d" % t, "rk%d" % t, "cnt%d" % t, "land%d" % t
         if t == 0:
             for b in range(2):
                 mm("sb%d" % b, b, "xu", 128 * b, "call", 0, 256, ["xuq"] + CALL)
         else:
             marks(t, 0)
             marks(t, 1)
-        above(t, 0)
-        if t:
             turn(t)
+        above(t, 0)
         above(t, 1)
-        quant("qind", "ind", 0, "ind", 0, 128, ["ind0", "ind1"], ["indq"])
+        quant("qind", "ind", 0, "ind", 0, 128, ["ind00", "ind01", "ind10", "ind11"], ["indq"])
         if t:
-            spread(t, (0, 1))
+            spread(t, (0, 1, 2))
         mm("cnt", 6, "ind", 0, "cm", 0, 128, ["indq", "cmq"])
-        ts("c16", T.ct[:, 0:2], ps(6, 0, 2), RND, RND, ALU.add, ALU.subtract, ["B6", "ct"], ["ct0"])
-        op("V", "crest", lambda e: e.tensor_tensor(T.ct[:, 4:6], ps(6, 0, 2), T.ct[:, 0:2], ALU.subtract), r=["B6", "ct0", "ct"], w=["ct1"])
-        quant("qct", arr, 16, "ct", 0, 128, ["ct", "ct0", "ct1"], ["arrown%d" % t])
-        send("snd_nq", ["arrown%d" % t], u8(T[arr + "q"][:, 16:18]),
-             lambda q: u8(T[arr + "q"][:, 2 * slot(r, q) - 2:2 * slot(r, q)]), "rn%d" % t)
-        send("snd_ns", ["arrown%d" % t], T[arr + "s"][:, 16:18],
-             lambda q: T[arr + "s"][:, 2 * slot(r, q) - 2:2 * slot(r, q)], "rn%d" % t)
-        op("X", "arr_n", None, w=["land" + arr], ext=(T.sem["rn%d" % t], 2 * lanes * (N - 1)))
-        if t:
-            spread(t, (2, 3))
-        else:
+        vcopy("cnt", T[cnt][:], ps(6, 0, 2), ["B6"], [cnt])
+        send("snd_n", [cnt], T[cnt][:], lambda q: T[land][:, 2 * slot(r, q) - 2:2 * slot(r, q)], "rn%d" % t)
+        op("X", "arr_n", None, w=[land], ext=(T.sem["rn%d" % t], lanes * (N - 1)))
+        ts("c16", T.o16[:], ps(6, 0, 2), RND, RND, ALU.add, ALU.subtract, ["B6"], ["o16"])
+        tt("crest", T.won[:], ps(6, 0, 2), T.o16[:], ALU.subtract, ["B6", "o16"], ["won"])
+        tt("ccap", T.o16[:], T.o16[:], T.cap[:], ALU.min, ["cap", "o16"], ["o16"])
+        for b in range(2):
+            acopy("own", T.kt[:, 512 * b + 3:512 * b + 512:4], T.ident[:], ["ident", "won"], ["ktr%d" % b], scale=T.won[:, b:b + 1])
+            acopy("own", T.kt[:, 512 * b + 1:512 * b + 512:4], T.ident[:], ["ident", "o16"], ["kto%d" % b], scale=T.o16[:, b:b + 1])
+        spread(t, (3,))
+        if t == 0:
+            op("G", "ktd", lambda e: e.iota(T.kt[64:65, 2:1024:4], [[-16, 16], [0, 16]], 240, 0, allow_small_or_imprecise_dtypes=True),
+               w=["ktd", "ktd2", "ktd3"])
+            op("G", "placen", lambda e: e.iota(T.placen[:], [[-2, 16]], 255, 0, allow_small_or_imprecise_dtypes=True), w=["placen"])
             for b in range(2):
                 mm("sa%d" % b, 2 + b, "call", 128 * b, "x", 0, 256, ["x"] + CALL)
         name_diff(0)
@@ -342,32 +346,45 @@ def rank_program(g, core, T, topo):
         name_run(0)
         name_at(0)
         name_run(1)
-        name_at(1)
         if t == 0:
-            eb_fill()
+            memset("kt64", T.kt[64:65, 258:1024:512], 0.0, ["ktd"])
+            memset("kt96", T.kt[96:97, 258:259], 176.0, ["ktd2"])
+            memset("kt96", T.kt[96:97, 770:771], 48.0, ["ktd3"])
+        if t == 0:
+            for b in range(4):
+                load("S", "z_eb", T.eb[:, 512 * b:512 * b + 512], T.zt[:], r=["zt", land], w=[EB[b]])
         if t == 1:
-            quant("qw", "w", 0, "wt", 0, 256, ["wt"], ["w"])
-            memset("ms_ohn", T.ohn[:], 0.0, ["ohn"])
-        for b in range(2):
-            mm("gain%d" % b, 4 + b, arr, 0, "ep", 128 * b, 128, ["land" + arr, "arr%d" % t, "arrown%d" % t, "epq"])
-        vcopy("gcopy0", T.kt[:, 0:512:4], ps(4, 0, 128), ["B4"], ["kta"])
-        acopy("gcopy1", T.kt[:, 512:1024:4], ps(5, 0, 128), ["B5"], ["ktb"])
-        quant("qkta", "kt", 0, "kt", 0, 128, ["kta", "ktexa", "ktc", "ktd"], ["ktqa"])
-        quant("qktb", "kt", 128, "kt", 512, 128, ["ktb", "ktexb", "ktc", "ktd"], ["ktqb"])
+            load("S", "ldw", T.wt[:, :], T.w[:, :], r=[land], w=["wt"])
+            load("S", "z_ohn", T.ohn[:], T.zt[:], r=["zt", land], w=["ohn"])
+        for b in (1, 0):
+            op("V", "tot", lambda e, b=b: e.tensor_reduce(T.tot[:, b:b + 1], T[land][:, b:14:2], AxisListType.X, ALU.add), r=[land], w=["tot%d" % b])
+        for b in (1, 0):
+            ts("offk", T.offk[:, 8 * b:8 * b + 8], T.gmask[:], T.tot[:, b:b + 1], None, ALU.mult, None, ["gmask", "tot%d" % b], ["offk%d" % b])
+        op("A", "gain1", lambda e: e.activation(T.kt[:, 512:1024:4], T.tab[:, 0:2048].indirect(T.offk[:, 8:16]), AF.Copy), r=TAB + ["offk1"], w=["ktb"])
+        op("V", "gain0", lambda e: e.tensor_copy(T.kt[:, 0:512:4], T.tab[:, 0:2048].indirect(T.offk[:, 0:8])), r=TAB + ["offk0"], w=["kta"])
+        name_at(1)
+        KC = ["ktc", "ktd", "ktc2", "ktd2", "ktd3"]
+        quant("qkta", "kt", 0, "kt", 0, 128, ["kta", "kto0", "ktr0"] + KC, ["ktqa"])
+        quant("qktb", "kt", 128, "kt", 512, 128, ["ktb", "kto1", "ktr1"] + KC, ["ktqb"])
         mm("kcol0", 6, "kt", 0, "wgt", 0, 128, ["ktqa", "wgtq"])
-        mm("krow", 7, "wgt", 0, "kt", 0, 256, ["ktqa", "ktqb", "wgtq"])
+        mm("krow0", 7, "wgt", 0, "kt", 0, 128, ["ktqa", "wgtq"])
         mm("kcol1", 4, "kt", 128, "wgt", 0, 128, ["ktqb", "wgtq"])
+        mm("krow1", 5, "wgt", 0, "kt", 128, 128, ["ktqb", "wgtq"])
         vcopy("kcc0", T.kcol[:, 0:1], ps(6, 0, 1), ["B6"], ["kcol0"])
-        ts("n16", T.nm[:, 24:26], T.name[:], RND, RND, ALU.add, ALU.subtract, ["name0", "name1", "nm"], ["nmhi"])
         vcopy("kcc1", T.kcol[:, 1:2], ps(4, 0, 1), ["B4"], ["kcol1"])
-        op("V", "nrest", lambda e: e.tensor_tensor(T.nm[:, 16:18], T.name[:], T.nm[:, 24:26], ALU.subtract), r=["name0", "name1", "nmhi", "nm"], w=["nmlo"])
-        quant("qnm", "nm", 0, "nm", 0, 130, ["nm", "nm_l", "nm_h", "nmlo", "nmhi"], ["nmq"])
-        for b in range(2):
-            op("A", "rank%d" % b, lambda e, b=b: e.activation(T["junk%d" % (2 + b)][:], ps(7, 0, 256), AF.Sign, bias=T.kcol[:, b:b + 1], scale=-1.0,
-                                                              accum_out=T[rk][:, b:b + 1]), r=["B7", "kcol%d" % b], w=["junk%d" % (2 + b), "%s.%d" % (rk, b)])
+        ts("n16", T.nm[:, 24:26], T.name[:], RND, RND, ALU.add, ALU.subtract, ["name0", "name1", "nm"], ["nmhi"])
+        tt("nrest", T.nm[:, 16:18], T.name[:], T.nm[:, 24:26], ALU.subtract, ["name0", "name1", "nmhi", "nm"], ["nmlo"])
+        quant("qnm", "nm", 0, "nm", 0, 130, ["nm", "nm2", "nm_l", "nm_h", "nmlo", "nmhi"], ["nmq"])
+        for h in range(2):
+            for b in range(2):
+                c = 2 * h + b
+                op("A", "rank%d" % c, lambda e, h=h, b=b, c=c: e.activation(T["junk%d" % c][:, 0:128], ps(7 - 2 * h, 0, 128), AF.Sign,
+                                                                            bias=T.kcol[:, b:b + 1], scale=-1.0, accum_out=T[rk][:, c:c + 1]),
+                   r=["B%d" % (7 - 2 * h), "kcol%d" % b], w=["junk%d" % c, "%s.%d" % (rk, c)])
         PL = ["place%d" % j for j in range(M)]
         for b in range(2):
-            ts("onehot%d" % b, T.oh[:, b:512:4], T.place[:], T[rk][:, b:b + 1], None, ALU.is_equal, None, ["%s.%d" % (rk, b)] + PL, ["oh%d" % b])
+            ts("onehot%d" % b, T.oh[:, b:512:4], T.place[:], T[rk][:, b:b + 1], T[rk][:, 2 + b:3 + b], ALU.subtract, ALU.is_equal,
+               [rk + ".%d" % b, rk + ".%d" % (2 + b)] + PL, ["oh%d" % b])
         quant("qoh", "oh", 0, "oh", 0, 128, ["oh0", "oh1"], ["ohq"])
         mm("lists", 5, "oh", 0, "nm", 0, 128, ["ohq", "nmq"])
         ts("offt", T[off][:, 0:1], ps(5, 4, 5), ps(5, 6, 7), None, ALU.add, None, ["B5"], [off + "t"])
@@ -380,22 +397,32 @@ def rank_program(g, core, T, topo):
         op("V", "candq", lambda e: e.tensor_copy(w32(T[win + "q"][:, 128:144]), w32(T.callq[:, 0:256]).indirect(T[off][:, 2:3])), r=CALL + [off + "c"], w=[win + ".cq"])
         op("A", "cands", lambda e: e.activation(T[win + "s"][:, 128:144], T.calls[:, 0:256].indirect(T[off][:, 2:3]), AF.Copy), r=CALL + [off + "c"], w=[win + ".cs"])
         if t + 1 < R:
-            ts("won", T.won[:], T[rk][:], 224.0, None, ALU.is_gt, None, [rk + ".0", rk + ".1"], ["won"])
-            op("V", "ex", lambda e: e.tensor_tensor(T.ex[:], T.ex[:], T.won[:], ALU.add), r=["won"], w=["ex"])
-            for b in range(2):
-                ts("ktex%d" % b, T.kt[:, 512 * b + 1:512 * b + 512:4], T.id256[:], T.ex[:, b:b + 1], None, ALU.mult, None, ["id256", "ex"], ["ktex" + "ab"[b]])
+            tt("won", T.won[:], T[rk][:, 0:2], T[rk][:, 2:4], ALU.add, [rk + ".%d" % c for c in range(4)], ["won"])
+            ts("won", T.won[:], T.won[:], 224.0, -4352.0, ALU.is_gt, ALU.mult, ["won"], ["won"])
+            ts("won", T.won[:], T.won[:], 256.0, None, ALU.add, None, ["won"], ["won"])
+            tt("cap", T.cap[:], T.cap[:], T.won[:], ALU.min, ["won", "cap"], ["cap"])
         else:
             for s in range(R):
                 for b in range(2):
-                    ts("ohn", T.ohn[:, 64 * s + b:64 * s + 64:4], T.placen[:], T["rk%d" % s][:, b:b + 1], None, ALU.is_equal, None,
-                       ["ohn", "placen", "rk%d.%d" % (s, b)], ["ohn%d%d" % (s, b)])
+                    rs = "rk%d" % s
+                    ts("ohn", T.ohn[:, 64 * s + b:64 * s + 64:4], T.placen[:], T[rs][:, b:b + 1], T[rs][:, 2 + b:3 + b], ALU.subtract, ALU.is_equal,
+                       ["ohn", "placen", rs + ".%d" % b, rs + ".%d" % (2 + b)], ["ohn%d%d" % (s, b)])
             quant("qohn", "ohn", 0, "ohn", 0, 128, ["ohn"] + ["ohn%d%d" % (s, b) for s in range(R) for b in range(2)], ["ohnq"])
             mm("sel0", 6, "nm", 0, "ohn", 0, 128, ["nmq", "ohnq"], True, False)
             mm("sel1", 6, "nm", 2, "ohn", 0, 128, ["nmq", "ohnq"], False, True)
             acopy("selrow", T.selrow[0:1, :], T.ps6[0:1, 0:48], ["B6"], ["selrow"])
             load("S", "st_sel", T.sel[0:1, :], T.selrow[0:1, :], r=["selrow"], w=["out.sel"])
         if t == 0:
-            vlist()
+            for b in range(4):
+                acopy("eb", T.eb[:, 512 * b + b:512 * b + 512:4], T.ident[:], ["ident"], [EB[b]])
+            memset("ms_fac", T.fac[:], 0.5, ["fac0", "fac1"])
+            op("V", "vtr", lambda e: e.transpose(T.vtr[:], T.vblk[:]), r=["vblk%d%d" % (c, b) for c in range(5) for b in range(2)], w=["vtr"])
+            memset("ms_fac0", T.fac[:, 0:80:5], 0.0, ["fac0"])
+            vcopy("offv", T.offv[:, 0:5], T.vtr[:, 0:160:32], ["vtr"], ["offv"])
+            memset("ms_fac1", T.fac[:, 1:80:5], 1.0, ["fac1"])
+            quant("qeb", "eb", 0, "eb", 0, 512, EB, ["ebq"])
+        if t == 1:
+            quant("qw", "w", 0, "wt", 0, 256, ["wt"], ["w"])
         WIN = ["land" + win, win + ".tq", win + ".ts", win + ".cq", win + ".cs", "offv"]
         op("V", "vinq", lambda e: e.tensor_copy(w32(T.vinq[:, 0:80]), w32(T[win + "q"][:, 0:144]).indirect(T.offv[:, 0:5])), r=WIN, w=["vin.q"])
         op("A", "vins", lambda e: e.activation(T.vins[:, 0:80], T[win + "s"][:, 0:144].indirect(T.offv[:, 0:5]), AF.Copy), r=WIN, w=["vin.s"])
@@ -403,7 +430,7 @@ def rank_program(g, core, T, topo):
             mm("dec%d" % b, 4 + b, "eb", 128 * b, "vin", 0, 128, ["ebq", "vin.q", "vin.s"])
         for b in range(4):
             op("V", "rec%d" % b, lambda e, b=b: e.tensor_tensor_scan(T["rec%d" % b][:], T.fac[:], ps(4 + b, 0, 80), 0.0, ALU.mult, ALU.add),
-               r=["B%d" % (4 + b), "fac"], w=["rec%d" % b])
+               r=["B%d" % (4 + b), "fac0", "fac1"], w=["rec%d" % b])
             acopy("cast%d" % b, T.h[:, 64 * (t + 1) + b:64 * (t + 2):4], T["rec%d" % b][:, 4:80:5], ["rec%d" % b], ["h%d" % b], scale=0.5)
         quant("qv", "v", 0, "h", 0, 128, HT + ["hu"], ["v"])
         zmul()

@@ -3,7 +3,6 @@ from concourse.mybir import dt, AluOpType as ALU, AxisListType, ActivationFuncti
 
 M, R, O = 16, 3, 2
 BFT, F32, I32, U16, COD, PLN = "bfloat16", "float32", "int32", "uint16", "float8_e4m3fn_x4", "uint8"
-
 SCRATCH = {}
 
 
@@ -17,36 +16,34 @@ def _codes(name, n):
 
 
 for _n, _w in (("ctile", 512), ("zt", 512), ("xt", 1024), ("xu", 1024), ("wt", 1024), ("h", 512), ("ind", 512), ("tab", 2048),
-               ("kt", 1024), ("oh", 512), ("ohn", 512), ("nm", 520), ("eb", 2048), ("cm", 512), ("wgt", 512),
-               ("ones", 128), ("ident", 128), ("place", 128), ("placen", 16),
-               ("junk0", 256), ("junk1", 256), ("junk2", 256), ("junk3", 256)):
+               ("kt", 1024), ("oh", 512), ("ohn", 512), ("nm", 520), ("eb", 2048), ("wgt", 512), ("gmask", 8),
+               ("ones", 128), ("ident", 128), ("place", 128), ("placen", 16), ("sg", 128), ("junk0", 256), ("junk1", 256)):
     _sb(_n, _w, BFT)
 for _n, _w in (("mrow", 256), ("d0", 256), ("d1", 256), ("run0", 256), ("run1", 256), ("kcol", 2), ("cap", 2), ("o16", 2),
-               ("tot", 2), ("gmask", 8), ("md", 3), ("step", 7), ("fac", 80), ("vrow", 80), ("vblk", 160), ("vtr", 160),
-               ("yt", 96), ("selrow", 48), ("name", 2), ("won", 2)):
+               ("tot", 2), ("md", 3), ("step", 7), ("fac", 80), ("low", 16), ("sq", 128),
+               ("vrow", 80), ("vblk", 160), ("vtr", 160), ("yt", 96), ("selrow", 48), ("name", 2), ("won", 2)):
     _sb(_n, _w, F32)
-for _b in range(4):
-    _sb("rec%d" % _b, 80, F32)
 for _t in range(R):
-    _sb("rk%d" % _t, 4, F32)
-for _t in range(R + 1):
-    _sb("mk%d" % _t, 64, F32)
+    _sb("rk%d" % _t, 2, F32)
+for _t in range(2):
+    _sb("mk%d" % _t, 96, F32)
     _sb("mt%d" % _t, 64, F32)
-for _n, _w in (("pn", 2), ("pl", 2), ("ph", 2), ("vi", 80), ("vi2", 80), ("gm", 8), ("gm2", 8), ("v16", 16)):
+for _n, _w in (("pn", 2), ("pl", 2), ("ph", 2), ("vi", 80), ("vi2", 80), ("v16", 16)):
     _sb(_n, _w, I32)
 _sb("offv", 6, U16)
 _sb("offk", 16, U16)
+_sb("offo", 2, U16)
 for _t in range(R):
     _sb("off%d" % _t, 4, U16)
     _sb("cnt%d" % _t, 2, BFT)
     _sb("land%d" % _t, 14, BFT)
     _codes("win%d" % _t, 144)
-for _n, _w in (("c", 128), ("call", 256), ("x", 256), ("xu", 256), ("w", 256), ("v", 128), ("ind", 128), ("kt", 256),
-               ("oh", 128), ("ohn", 128), ("nm", 130), ("eb", 512), ("cm", 128), ("wgt", 128), ("vin", 128)):
+    _codes("v%d" % _t, 128)
+for _n, _w in (("c", 128), ("call", 256), ("x", 256), ("xu", 256), ("w", 256), ("vu", 128), ("vo", 48), ("ind", 128), ("kt", 256),
+               ("oh", 128), ("ohn", 128), ("nm", 130), ("eb", 512), ("wgt", 128), ("vin", 128)):
     _codes(_n, _w)
 for _b in range(8):
     SCRATCH["ps%d" % _b] = ("psum", [128, 512], F32)
-
 SEMAPHORES = ["rc"] + ["rn%d" % t for t in range(R)] + ["rt%d" % t for t in range(R)] + ["ls"] + ["e%d" % i for i in range(140)]
 
 
@@ -128,7 +125,18 @@ def rank_program(g, core, T, topo):
     cores = list(T.cores)
     N = len(cores)
     P = {"ops": [], "tags": {}}
-    others = [q for q in range(N) if q != r]
+    chip = [topo.chip(q) for q in cores]
+    ways = {"far": [], "plane": [], "mate": []}
+    for d in range(1, N):
+        q = r ^ d
+        way = "mate" if topo.mates(chip[r], chip[q]) else "plane" if topo.same_plane(chip[r], chip[q]) else "far"
+        ways[way].append(q)
+    others = []
+    while ways["far"] or ways["plane"]:
+        for way in ("far", "plane"):
+            others += ways[way][:1]
+            del ways[way][:1]
+    others += ways["mate"]
     mask = 0xFFFF
     for q in others:
         mask &= topo.mask(core, cores[q])
@@ -195,24 +203,23 @@ def rank_program(g, core, T, topo):
     place_of = {k: j for j, k in enumerate(order)}
     HT = ["h0", "h1", "h2", "h3"]
     EB = ["eb0", "eb1", "eb2", "eb3"]
+    PL = ["place%d" % j for j in range(M)]
     RND = 1.5 * 2.0 ** 27
+    CV = 96
+    NV = 5 * M
 
     load("S", "ldc", T.ctile[:, 0:128], T.c[:, :], w=["ctile"])
     load("A", "ldx", T.xt[:, :], T.x[:, :], w=["xt"])
-    memset("ms_h", T.h[:], 0.0, HT + ["hu"])
-    load("S", "ldu", T.h[:, 60:64], T.u[:, 0:4], w=["hu"])
     memset("ms_c", T.ctile[:, 128:512], 0.0, ["ctile0"])
     memset("ms_ones", T.ones[:], 1.0, ["ones"])
+    memset("ms_h", T.h[:], 0.0, HT + ["hu", "hc0", "hc1"])
+    memset("ms_h1", T.h[:, 4 * CV:4 * CV + 2], 1.0, ["hc0"])
+    memset("ms_h2", T.h[:, 4 * CV + 6:4 * CV + 8], 1.0, ["hc1"])
+    load("S", "ldu", T.h[:, 4 * NV:4 * NV + 4], T.u[:, 0:4], w=["hu"])
     memset("ms_zt", T.zt[:], 0.0, ["zt"])
-    quant("qzv", "vin", 0, "zt", 0, 128, ["zt"], ["vin.q", "vin.s"])
-    memset("ms_cm", T.cm[:], 0.0, ["cm0", "cm1", "cm2"])
-    memset("ms_kt", T.kt[:], 0.0, ["kta", "ktb", "kto0", "kto1", "ktr0", "ktr1", "ktc", "ktd"])
-    memset("ms_cm1", T.cm[:, 0:2], 1.0, ["cm1"])
-    memset("ms_cm2", T.cm[:, 6:8], 1.0, ["cm2"])
     op("G", "pn", lambda e: e.iota(T.pn[:], [[128, 2]], 0, 1), w=["pn"])
     op("G", "vi", lambda e: e.iota(T.vi[:], [[4, 2], [16, 8], [17, 5]], 256 - 17 - 16 * r, 0), w=["vi"])
     op("G", "v16", lambda e: e.iota(T.v16[:], [[1, 16]], 0, 0), w=["v16"])
-    op("G", "gm", lambda e: e.iota(T.gm[:], [[-16, 8]], 0, 1), w=["gm"])
     op("G", "ident", lambda e: e.affine_select(T.ident[:], T.ones[:], [[-1, 128]], ALU.is_equal, 0.0, 0, 1), r=["ones"], w=["ident"])
 
     quant("qc", "c", 0, "ctile", 0, 128, ["ctile", "ctile0"], ["c"])
@@ -224,167 +231,196 @@ def rank_program(g, core, T, topo):
     CALL = ["call", "own.q", "own.s"]
 
     for j in range(M):
-        acopy("place", T.place[:, j:128:16], T.ones[:, 0:8], ["ones"], ["place%d" % j], scale=255.0 - 2.0 * order[j])
-    acopy("z_nm", T.nm[:, 0:512], T.zt[:], ["zt"], ["nm", "nmlo", "nmhi"])
+        acopy("place", T.place[:, j:128:16], T.ones[:, 0:8], ["ones"], [PL[j]], scale=255.0 - 2.0 * order[j])
+    memset("ms_kt", T.kt[:], 0.0, ["kta", "ktb", "kto0", "kto1", "ktr0", "ktr1", "ktc", "ktd"])
+    for t in range(2):
+        memset("ms_mk%d" % t, T["mk%d" % t][:, 32:96], 0.0, ["mk%d.0" % t, "mk%d.1" % t])
     for a in range(4):
         for b in range(2):
             (vcopy if b else acopy)("xu", T.xu[:, 512 * b + 128 * a:512 * b + 128 * a + 128], T.xt[:, 256 * a + 128 * b:256 * a + 128 * b + 128],
                                     ["xt"], ["xu%d%d" % (a, b)])
-    acopy("z_oh", T.oh[:], T.zt[:], ["zt"], ["oh0", "oh1"])
-    quant("qx", "x", 0, "xt", 0, 256, ["xt"], ["x"])
-    quant("qv", "v", 0, "h", 0, 128, HT + ["hu"], ["v"])
-    memset("z_nm2", T.nm[:, 512:520], 0.0, ["nm2"])
-    for t in range(R + 1):
-        memset("ms_mk%d" % t, T["mk%d" % t][:], 0.0, ["mk%d.0" % t, "mk%d.1" % t])
+    quant("qv", "vu", 0, "h", 0, 128, HT + ["hu", "hc0", "hc1"], ["vu"])
     quant("qxu", "xu", 0, "xu", 0, 256, ["xu%d%d" % (a, b) for a in range(4) for b in range(2)], ["xuq"])
-    quant("qcm", "cm", 0, "cm", 0, 128, ["cm0", "cm1", "cm2"], ["cmq"])
-    for e_, v in enumerate((256.0, 256.0, 1.0, 256.0)):
-        memset("ms_wgt", T.wgt[:, e_:512:4], v, ["wgt%d" % e_])
+    acopy("z_nm", T.nm[:, 0:512], T.zt[:], ["zt"], ["nm", "nmlo", "nmhi"])
+    acopy("z_oh", T.oh[:], T.zt[:], ["zt"], ["oh0", "oh1"])
+    ts("pl", T.pl[:], T.pn[:], 15, None, ALU.bitwise_and, None, ["pn"], ["pl"])
+    ts("vi2", T.vi2[:], T.vi[:], 127, None, ALU.bitwise_and, None, ["vi"], ["vi2"])
+    for d in range(3):
+        ts("md", T.md[:, d:d + 1], T.pl[:, 0:1], 3.0 + d, None, ALU.is_equal, None, ["pl"], ["md%d" % d])
+    vcopy("vrow", T.vrow[:], T.vi2[:], ["vi2"], ["vrow"])
+    for k in range(7):
+        acopy("step", T.step[:, k:k + 1], T.md[:, 1 + k // 4:2 + k // 4], ["md%d" % (1 + k // 4)], ["step%d" % k], scale=16.0 * 2 ** k)
+    quant("qx", "x", 0, "xt", 0, 256, ["xt"], ["x"])
+    memset("ms_wgt", T.wgt[:], 256.0, ["wgt"])
+    memset("ms_wgt", T.wgt[:, 2:512:4], 1.0, ["wgt"])
+    op("G", "ktc", lambda e: e.iota(T.kt[32:33, 2:1024:4], [[0, 16], [-1, 16]], 15, 0, allow_small_or_imprecise_dtypes=True), w=["ktc", "ktc2"])
+    op("G", "ktd", lambda e: e.iota(T.kt[64:65, 2:1024:4], [[-16, 16], [0, 16]], 240, 0, allow_small_or_imprecise_dtypes=True),
+       w=["ktd", "ktd2", "ktd3"])
+    op("G", "gmask0", lambda e: e.affine_select(T.gmask[:], T.ones[:, 0:8], [[-16, 8]], ALU.is_ge, 0.0, 0, 1), r=["ones"], w=["gmask"])
+    op("G", "gmask1", lambda e: e.affine_select(T.gmask[:], T.gmask[:], [[16, 8]], ALU.is_ge, 0.0, 15, -1), r=["gmask"], w=["gmask"])
 
-    def zmul():
+    def zmul(v):
         for b in range(2):
-            mm("z%d" % b, 4 + b, "xu", 128 * b, "v", 0, 128, ["xuq", "v"])
+            mm("z%d" % b, 4 + b, "xu", 128 * b, v, 0, 128, ["xuq", v])
+
+    def mk(t, b):
+        return T["mk%d" % (t % 2)][:, 32 * b + 32:32 * b + 33]
 
     def marks(t, b):
-        op("V", "mark%d" % b, lambda e: e.tensor_reduce(T["mk%d" % t][:, 32 * b:32 * b + 1], ps(4 + b, 15, 16 + M * t), AxisListType.X, ALU.max),
-           r=["B%d" % (4 + b)], w=["mk%d.%d" % (t, b)])
+        q = "mk%d.%d" % (t % 2, b)
+        if t == 0:
+            vcopy("mark%d" % b, mk(0, b), ps(4 + b, NV, NV + 1), ["B%d" % (4 + b)], [q])
+        else:
+            op("V", "mark%d" % b, lambda e: e.tensor_tensor_scan(T["mk%d" % (t % 2)][:, 32 * b + 33 - M:32 * b + 33], T["ps%d" % (4 + b)][:, 4:NV:5],
+                                                                 T.low[:], mk(t - 1, b), ALU.max, ALU.max),
+               r=["B%d" % (4 + b), "low", "mk%d.%d" % ((t - 1) % 2, b)], w=[q])
 
     def turn(t):
-        op("V", "turn", lambda e: e.transpose(T["mt%d" % t][:], T["mk%d" % t][:]), r=["mk%d.0" % t, "mk%d.1" % t], w=["mt%d" % t])
+        op("V", "turn", lambda e: e.transpose(T["mt%d" % (t % 2)][:], T["mk%d" % (t % 2)][:, 32:96]),
+           r=["mk%d.0" % (t % 2), "mk%d.1" % (t % 2)], w=["mt%d" % (t % 2)])
 
     def spread(t, aa):
         for a in aa:
-            op("G", "spread%d" % a, lambda e, a=a: e.partition_broadcast(T.mrow[:, 64 * a:64 * a + 64], T["mt%d" % t][32 * a:32 * a + 1, :], 128),
-               r=["mt%d" % t], w=["mrow%d" % a])
+            op("G", "spread%d" % a, lambda e, a=a: e.partition_broadcast(T.mrow[:, 64 * a:64 * a + 64], T["mt%d" % (t % 2)][32 * a:32 * a + 1, :], 128),
+               r=["mt%d" % (t % 2)], w=["mrow%d" % a])
 
-    zmul()
-    ts("pl", T.pl[:], T.pn[:], 15, None, ALU.bitwise_and, None, ["pn"], ["pl"])
-    ts("vi2", T.vi2[:], T.vi[:], 127, None, ALU.bitwise_and, None, ["vi"], ["vi2"])
+    zmul("vu")
     marks(0, 0)
     marks(0, 1)
-    vcopy("vrow", T.vrow[:], T.vi2[:], ["vi2"], ["vrow"])
+    quant("qwgt", "wgt", 0, "wgt", 0, 128, ["wgt"], ["wgtq"])
     turn(0)
-    quant("qwgt", "wgt", 0, "wgt", 0, 128, ["wgt%d" % e_ for e_ in range(4)], ["wgtq"])
-    op("G", "ktc", lambda e: e.iota(T.kt[32:33, 2:1024:4], [[0, 16], [-1, 16]], 15, 0, allow_small_or_imprecise_dtypes=True), w=["ktc", "ktc2"])
-    spread(0, (0, 1, 2))
-    for d in range(3):
-        ts("md", T.md[:, d:d + 1], T.pl[:, 0:1], 3.0 + d, None, ALU.is_equal, None, ["pl"], ["md%d" % d])
-    memset("ms_cap", T.cap[:], 256.0, ["cap"])
+    spread(0, (0, 1, 2, 3))
     ts("tab", T.tab[:, 0:16], T.v16[:], T.md[:, 0:1], None, ALU.mult, None, ["v16", "md0"], ["tab0"])
-    for k in range(7):
-        ts("step", T.step[:, k:k + 1], T.md[:, 1 + k // 4:2 + k // 4], 16.0 * 2 ** k, None, ALU.mult, None, ["md%d" % (1 + k // 4)], ["step%d" % k])
+    memset("ms_cap", T.cap[:], 256.0, ["cap"])
     for k in range(5):
         m = 16 << k
         ts("tab", T.tab[:, m:2 * m], T.tab[:, 0:m], T.step[:, k:k + 1], None, ALU.add, None, ["tab%d" % j for j in range(k + 1)] + ["step%d" % k], ["tab%d" % (k + 1)])
+    TOP = 256 * (N - 1) + 16
     TAB = ["tab%d" % j for j in range(8)]
     memset("kt32", T.kt[32:33, 130:1024:512], 0.0, ["ktc"])
     memset("kt96", T.kt[96:97, 130:1024:512], 15.0, ["ktc2"])
-    ts("gm2", T.gm2[:], T.gm[:], 4, None, ALU.arith_shift_right, None, ["gm"], ["gm2"])
-    ts("ph", T.ph[:], T.pn[:], 240, None, ALU.bitwise_and, None, ["pn"], ["ph"])
-    vcopy("nm_l", T.nm[:, 0:2], T.pl[:], ["pl", "nm"], ["nm_l"])
-    ts("gmask", T.gmask[:], T.gm2[:], 0.0, None, ALU.is_equal, None, ["gm2"], ["gmask"])
-    vcopy("nm_h", T.nm[:, 8:10], T.ph[:], ["ph", "nm"], ["nm_h"])
+    memset("kt64", T.kt[64:65, 258:1024:512], 0.0, ["ktd"])
+    memset("kt96", T.kt[96:97, 258:259], 176.0, ["ktd2"])
+    memset("kt96", T.kt[96:97, 770:771], 48.0, ["ktd3"])
     for k in range(M):
         acopy("vrowk", T.vrow[:, 5 * k:5 * k + 1], T.ones[:, 0:1], ["vrow", "ones"], ["vrow.%d" % k], scale=float(128 + place_of[k]))
-    for c in range(5):
-        for b in range(2):
-            acopy("vblk", T.vblk[:, 32 * c + 16 * b:32 * c + 16 * b + 16], T.vrow[:, 16 * c:16 * c + 16],
-                  ["vrow"] + ["vrow.%d" % k for k in range(M)], ["vblk%d%d" % (c, b)])
     for k in (5, 6):
-        op("A", "tab", lambda e, m=16 << k, k=k: e.activation(T.tab[:, m:2 * m], T.tab[:, 0:m], AF.Identity, bias=T.step[:, k:k + 1]),
+        op("A", "tab", lambda e, m=16 << k, k=k: e.activation(T.tab[:, m:min(2 * m, TOP)], T.tab[:, 0:min(m, TOP - m)], AF.Identity, bias=T.step[:, k:k + 1]),
            r=["tab%d" % j for j in range(k + 1)] + ["step%d" % k], w=["tab%d" % (k + 1)])
 
-    def above(t, b):
-        for k in range(2):
-            ts("above", T.ind[:, 2 * k + b:512:4], ps(b, 128 * k, 128 * k + 128), T["mk%d" % t][:, 32 * b:32 * b + 1], None, ALU.is_gt, None,
-               ["B%d" % b, "mk%d.%d" % (t, b)], ["ind%d%d" % (b, k)])
+    def above(t, b, k):
+        ts("above", T.ind[:, 2 * k + b:512:4], ps(b, 128 * k, 128 * k + 128), mk(t, b), None, ALU.is_gt, None,
+           ["B%d" % b, "mk%d.%d" % (t % 2, b)], ["ind%d%d" % (b, k)])
 
-    def name_diff(b):
-        tt("diff%d" % b, T["d%d" % b][:], ps(2 + b, 0, 256), T.mrow[:], ALU.subtract, ["B%d" % (2 + b)] + ["mrow%d" % a for a in range(4)], ["d%d" % b])
+    def above_a(t):
+        op("A", "sgn", lambda e: e.activation(T.sg[:], T.sq[:], AF.Sign, bias=mk(t, 0), scale=-1.0), r=["sq", "mk%d.0" % (t % 2)], w=["sg"])
+        op("A", "neg", lambda e: e.activation(T.ind[:, 2:512:4], T.sg[:], AF.Relu, scale=-1.0), r=["sg"], w=["ind01"])
 
-    def name_run(b):
-        op("V", "run%d" % b, lambda e: e.tensor_tensor_scan(T["run%d" % b][:], T["d%d" % b][:], T["d%d" % b][:], -1e29, ALU.max, ALU.max),
-           r=["d%d" % b], w=["run%d" % b])
+    def pieces(what, b, lo, hi):
+        return ["%s%d.%d" % (what, b, h) for h in range(lo // 64, hi // 64)]
+
+    def name_diff(b, lo, hi):
+        tt("diff%d" % b, T["d%d" % b][:, lo:hi], ps(2 + b, lo, hi), T.mrow[:, lo:hi], ALU.subtract,
+           ["B%d" % (2 + b)] + ["mrow%d" % a for a in range(lo // 64, hi // 64)], pieces("d", b, lo, hi))
+
+    def name_run(b, lo, hi):
+        first = T["run%d" % b][:, lo - 1:lo] if lo else -1e29
+        op("V", "run%d" % b, lambda e: e.tensor_tensor_scan(T["run%d" % b][:, lo:hi], T["d%d" % b][:, lo:hi], T["d%d" % b][:, lo:hi], first, ALU.max, ALU.max),
+           r=pieces("d", b, lo, hi) + (pieces("run", b, 0, lo) if lo else []), w=pieces("run", b, lo, hi))
 
     def name_at(b):
         op("A", "name%d" % b, lambda e: e.activation(T["junk%d" % b][:], T["run%d" % b][:], AF.Sign, bias=T["run%d" % b][:, 255:256], scale=-1.0,
-                                                     accum_out=T.name[:, b:b + 1]), r=["run%d" % b], w=["junk%d" % b, "name%d" % b])
+                                                     accum_out=T.name[:, b:b + 1]), r=pieces("run", b, 0, 256), w=["junk%d" % b, "name%d" % b])
+
+    def pick_out(t):
+        v = "v%d" % t
+        op("V", "outq", lambda e: e.tensor_copy(w32(T.voq[:, M * t:M * t + M]), w32(T[v + "q"][:, 0:128]).indirect(T.offo[:, 0:1])), r=[v, "offo"], w=["vo.q%d" % t])
+        op("A", "outs", lambda e: e.activation(T.vos[:, M * t:M * t + M], T[v + "s"][:, 0:128].indirect(T.offo[:, 0:1]), AF.Copy), r=[v, "offo"], w=["vo.s%d" % t])
+
+    def products(t):
+        v = "v%d" % t
+        for o in range(O):
+            mm("y%d" % o, 6 + o, "w", 128 * o, v, 0, 128, ["w", v])
+        for o in range(O):
+            (vcopy if o else acopy)("yc%d" % o, T.yt[:, R * M * o + M * t:R * M * o + M * t + M], T["ps%d" % (6 + o)][:, 4:NV:5],
+                                    ["B%d" % (6 + o)], ["yt%d%d" % (t, o)])
 
     def one_round(t):
         win, off, rk, cnt, land = "win%d" % t, "off%d" % t, "rk%d" % t, "cnt%d" % t, "land%d" % t
         if t == 0:
             for b in range(2):
                 mm("sb%d" % b, b, "xu", 128 * b, "call", 0, 256, ["xuq"] + CALL)
+            for b in range(2):
+                for k in range(2):
+                    above(t, b, k)
         else:
             marks(t, 0)
+            above_a(t)
+            above(t, 0, 0)
             marks(t, 1)
             turn(t)
-        above(t, 0)
-        above(t, 1)
+            above(t, 1, 0)
+            above(t, 1, 1)
         quant("qind", "ind", 0, "ind", 0, 128, ["ind00", "ind01", "ind10", "ind11"], ["indq"])
         if t:
-            spread(t, (0, 1, 2))
-        mm("cnt", 6, "ind", 0, "cm", 0, 128, ["indq", "cmq"])
-        vcopy("cnt", T[cnt][:], ps(6, 0, 2), ["B6"], [cnt])
+            spread(t, (0, 1))
+        mm("cnt", 6, "ind", 0, "vu", 0, 128, ["indq", "vu"])
+        vcopy("cnt", T[cnt][:], ps(6, CV, CV + 2), ["B6"], [cnt])
         send("snd_n", [cnt], T[cnt][:], lambda q: T[land][:, 2 * slot(r, q) - 2:2 * slot(r, q)], "rn%d" % t)
         op("X", "arr_n", None, w=[land], ext=(T.sem["rn%d" % t], lanes * (N - 1)))
-        ts("c16", T.o16[:], ps(6, 0, 2), RND, RND, ALU.add, ALU.subtract, ["B6"], ["o16"])
-        tt("crest", T.won[:], ps(6, 0, 2), T.o16[:], ALU.subtract, ["B6", "o16"], ["won"])
+        ts("c16", T.o16[:], ps(6, CV, CV + 2), RND, RND, ALU.add, ALU.subtract, ["B6"], ["o16"])
+        tt("crest", T.won[:], ps(6, CV, CV + 2), T.o16[:], ALU.subtract, ["B6", "o16"], ["won"])
         tt("ccap", T.o16[:], T.o16[:], T.cap[:], ALU.min, ["cap", "o16"], ["o16"])
         for b in range(2):
             acopy("own", T.kt[:, 512 * b + 3:512 * b + 512:4], T.ident[:], ["ident", "won"], ["ktr%d" % b], scale=T.won[:, b:b + 1])
             acopy("own", T.kt[:, 512 * b + 1:512 * b + 512:4], T.ident[:], ["ident", "o16"], ["kto%d" % b], scale=T.o16[:, b:b + 1])
-        spread(t, (3,))
-        if t == 0:
-            op("G", "ktd", lambda e: e.iota(T.kt[64:65, 2:1024:4], [[-16, 16], [0, 16]], 240, 0, allow_small_or_imprecise_dtypes=True),
-               w=["ktd", "ktd2", "ktd3"])
+        if t:
+            spread(t, (2, 3))
+        else:
             op("G", "placen", lambda e: e.iota(T.placen[:], [[-2, 16]], 255, 0, allow_small_or_imprecise_dtypes=True), w=["placen"])
             for b in range(2):
                 mm("sa%d" % b, 2 + b, "call", 128 * b, "x", 0, 256, ["x"] + CALL)
-        name_diff(0)
-        name_diff(1)
-        name_run(0)
+        for lo, hi in (((0, 128), (128, 192), (192, 256)) if t else ((0, 256),)):
+            for b in range(2):
+                name_diff(b, lo, hi)
+            for b in range(2):
+                name_run(b, lo, hi)
         name_at(0)
-        name_run(1)
-        if t == 0:
-            memset("kt64", T.kt[64:65, 258:1024:512], 0.0, ["ktd"])
-            memset("kt96", T.kt[96:97, 258:259], 176.0, ["ktd2"])
-            memset("kt96", T.kt[96:97, 770:771], 48.0, ["ktd3"])
         if t == 0:
             for b in range(4):
                 load("S", "z_eb", T.eb[:, 512 * b:512 * b + 512], T.zt[:], r=["zt", land], w=[EB[b]])
         if t == 1:
             load("S", "ldw", T.wt[:, :], T.w[:, :], r=[land], w=["wt"])
             load("S", "z_ohn", T.ohn[:], T.zt[:], r=["zt", land], w=["ohn"])
-        for b in (1, 0):
+        for b in range(2):
             op("V", "tot", lambda e, b=b: e.tensor_reduce(T.tot[:, b:b + 1], T[land][:, b:14:2], AxisListType.X, ALU.add), r=[land], w=["tot%d" % b])
-        for b in (1, 0):
+        for b in range(2):
             ts("offk", T.offk[:, 8 * b:8 * b + 8], T.gmask[:], T.tot[:, b:b + 1], None, ALU.mult, None, ["gmask", "tot%d" % b], ["offk%d" % b])
-        op("A", "gain1", lambda e: e.activation(T.kt[:, 512:1024:4], T.tab[:, 0:2048].indirect(T.offk[:, 8:16]), AF.Copy), r=TAB + ["offk1"], w=["ktb"])
-        op("V", "gain0", lambda e: e.tensor_copy(T.kt[:, 0:512:4], T.tab[:, 0:2048].indirect(T.offk[:, 0:8])), r=TAB + ["offk0"], w=["kta"])
+        op("A", "gain1", lambda e: e.activation(T.kt[:, 512:1024:4], T.tab[:, 0:TOP].indirect(T.offk[:, 8:16]), AF.Copy), r=TAB + ["offk1"], w=["ktb"])
+        op("V", "gain0", lambda e: e.tensor_copy(T.kt[:, 0:512:4], T.tab[:, 0:TOP].indirect(T.offk[:, 0:8])), r=TAB + ["offk0"], w=["kta"])
         name_at(1)
         KC = ["ktc", "ktd", "ktc2", "ktd2", "ktd3"]
         quant("qkta", "kt", 0, "kt", 0, 128, ["kta", "kto0", "ktr0"] + KC, ["ktqa"])
         quant("qktb", "kt", 128, "kt", 512, 128, ["ktb", "kto1", "ktr1"] + KC, ["ktqb"])
         mm("kcol0", 6, "kt", 0, "wgt", 0, 128, ["ktqa", "wgtq"])
-        mm("krow0", 7, "wgt", 0, "kt", 0, 128, ["ktqa", "wgtq"])
+        mm("krow", 7, "wgt", 0, "kt", 0, 256, ["ktqa", "ktqb", "wgtq"])
         mm("kcol1", 4, "kt", 128, "wgt", 0, 128, ["ktqb", "wgtq"])
-        mm("krow1", 5, "wgt", 0, "kt", 128, 128, ["ktqb", "wgtq"])
+        if t == 0:
+            ts("ph", T.ph[:], T.pn[:], 240, None, ALU.bitwise_and, None, ["pn"], ["ph"])
+            vcopy("nm_l", T.nm[:, 0:2], T.pl[:], ["pl", "nm"], ["nm_l"])
         vcopy("kcc0", T.kcol[:, 0:1], ps(6, 0, 1), ["B6"], ["kcol0"])
-        vcopy("kcc1", T.kcol[:, 1:2], ps(4, 0, 1), ["B4"], ["kcol1"])
+        if t == 0:
+            vcopy("nm_h", T.nm[:, 8:10], T.ph[:], ["ph", "nm"], ["nm_h"])
+            memset("z_nm2", T.nm[:, 512:520], 0.0, ["nm2"])
         ts("n16", T.nm[:, 24:26], T.name[:], RND, RND, ALU.add, ALU.subtract, ["name0", "name1", "nm"], ["nmhi"])
+        vcopy("kcc1", T.kcol[:, 1:2], ps(4, 0, 1), ["B4"], ["kcol1"])
         tt("nrest", T.nm[:, 16:18], T.name[:], T.nm[:, 24:26], ALU.subtract, ["name0", "name1", "nmhi", "nm"], ["nmlo"])
         quant("qnm", "nm", 0, "nm", 0, 130, ["nm", "nm2", "nm_l", "nm_h", "nmlo", "nmhi"], ["nmq"])
-        for h in range(2):
-            for b in range(2):
-                c = 2 * h + b
-                op("A", "rank%d" % c, lambda e, h=h, b=b, c=c: e.activation(T["junk%d" % c][:, 0:128], ps(7 - 2 * h, 0, 128), AF.Sign,
-                                                                            bias=T.kcol[:, b:b + 1], scale=-1.0, accum_out=T[rk][:, c:c + 1]),
-                   r=["B%d" % (7 - 2 * h), "kcol%d" % b], w=["junk%d" % c, "%s.%d" % (rk, c)])
-        PL = ["place%d" % j for j in range(M)]
         for b in range(2):
-            ts("onehot%d" % b, T.oh[:, b:512:4], T.place[:], T[rk][:, b:b + 1], T[rk][:, 2 + b:3 + b], ALU.subtract, ALU.is_equal,
-               [rk + ".%d" % b, rk + ".%d" % (2 + b)] + PL, ["oh%d" % b])
+            op("A", "rank%d" % b, lambda e, b=b: e.activation(T["junk%d" % b][:], ps(7, 0, 256), AF.Sign, bias=T.kcol[:, b:b + 1], scale=-1.0,
+                                                              accum_out=T[rk][:, b:b + 1]), r=["B7", "kcol%d" % b], w=["junk%d" % b, "%s.%d" % (rk, b)])
+        for b in range(2):
+            ts("onehot%d" % b, T.oh[:, b:512:4], T.place[:], T[rk][:, b:b + 1], None, ALU.is_equal, None, [rk + ".%d" % b] + PL, ["oh%d" % b])
         quant("qoh", "oh", 0, "oh", 0, 128, ["oh0", "oh1"], ["ohq"])
         mm("lists", 5, "oh", 0, "nm", 0, 128, ["ohq", "nmq"])
         ts("offt", T[off][:, 0:1], ps(5, 4, 5), ps(5, 6, 7), None, ALU.add, None, ["B5"], [off + "t"])
@@ -397,61 +433,69 @@ def rank_program(g, core, T, topo):
         op("V", "candq", lambda e: e.tensor_copy(w32(T[win + "q"][:, 128:144]), w32(T.callq[:, 0:256]).indirect(T[off][:, 2:3])), r=CALL + [off + "c"], w=[win + ".cq"])
         op("A", "cands", lambda e: e.activation(T[win + "s"][:, 128:144], T.calls[:, 0:256].indirect(T[off][:, 2:3]), AF.Copy), r=CALL + [off + "c"], w=[win + ".cs"])
         if t + 1 < R:
-            tt("won", T.won[:], T[rk][:, 0:2], T[rk][:, 2:4], ALU.add, [rk + ".%d" % c for c in range(4)], ["won"])
-            ts("won", T.won[:], T.won[:], 224.0, -4352.0, ALU.is_gt, ALU.mult, ["won"], ["won"])
+            ts("won", T.won[:], T[rk][:], 224.0, -4352.0, ALU.is_gt, ALU.mult, [rk + ".0", rk + ".1"], ["won"])
             ts("won", T.won[:], T.won[:], 256.0, None, ALU.add, None, ["won"], ["won"])
             tt("cap", T.cap[:], T.cap[:], T.won[:], ALU.min, ["won", "cap"], ["cap"])
         else:
             for s in range(R):
                 for b in range(2):
                     rs = "rk%d" % s
-                    ts("ohn", T.ohn[:, 64 * s + b:64 * s + 64:4], T.placen[:], T[rs][:, b:b + 1], T[rs][:, 2 + b:3 + b], ALU.subtract, ALU.is_equal,
-                       ["ohn", "placen", rs + ".%d" % b, rs + ".%d" % (2 + b)], ["ohn%d%d" % (s, b)])
+                    ts("ohn", T.ohn[:, 64 * s + b:64 * s + 64:4], T.placen[:], T[rs][:, b:b + 1], None, ALU.is_equal, None,
+                       ["ohn", "placen", rs + ".%d" % b], ["ohn%d%d" % (s, b)])
             quant("qohn", "ohn", 0, "ohn", 0, 128, ["ohn"] + ["ohn%d%d" % (s, b) for s in range(R) for b in range(2)], ["ohnq"])
             mm("sel0", 6, "nm", 0, "ohn", 0, 128, ["nmq", "ohnq"], True, False)
             mm("sel1", 6, "nm", 2, "ohn", 0, 128, ["nmq", "ohnq"], False, True)
             acopy("selrow", T.selrow[0:1, :], T.ps6[0:1, 0:48], ["B6"], ["selrow"])
             load("S", "st_sel", T.sel[0:1, :], T.selrow[0:1, :], r=["selrow"], w=["out.sel"])
         if t == 0:
+            for c in range(5):
+                for b in range(2):
+                    acopy("vblk", T.vblk[:, 32 * c + 16 * b:32 * c + 16 * b + 16], T.vrow[:, 16 * c:16 * c + 16],
+                          ["vrow"] + ["vrow.%d" % k for k in range(M)], ["vblk%d%d" % (c, b)])
             for b in range(4):
-                acopy("eb", T.eb[:, 512 * b + b:512 * b + 512:4], T.ident[:], ["ident"], [EB[b]])
+                acopy("eb", T.eb[:, 512 * b + b:512 * b + 512:4], T.ident[:], ["ident"], [EB[b]], scale=0.5)
+            acopy("sq", T.sq[:], ps(0, 128, 256), ["B0"], ["sq"])
+            quant("qzv", "vin", 0, "zt", 0, 128, ["zt"], ["vin.q", "vin.s"])
+            memset("ms_low", T.low[:], -1e29, ["low"])
             memset("ms_fac", T.fac[:], 0.5, ["fac0", "fac1"])
-            op("V", "vtr", lambda e: e.transpose(T.vtr[:], T.vblk[:]), r=["vblk%d%d" % (c, b) for c in range(5) for b in range(2)], w=["vtr"])
+            ts("offo", T.offo[:], T.pl[:], 5.0, 4.0, ALU.mult, ALU.add, ["pl"], ["offo"])
             memset("ms_fac0", T.fac[:, 0:80:5], 0.0, ["fac0"])
-            vcopy("offv", T.offv[:, 0:5], T.vtr[:, 0:160:32], ["vtr"], ["offv"])
             memset("ms_fac1", T.fac[:, 1:80:5], 1.0, ["fac1"])
+            op("V", "vtr", lambda e: e.transpose(T.vtr[:], T.vblk[:]), r=["vblk%d%d" % (c, b) for c in range(5) for b in range(2)], w=["vtr"])
+            vcopy("offv", T.offv[:, 0:5], T.vtr[:, 0:160:32], ["vtr"], ["offv"])
             quant("qeb", "eb", 0, "eb", 0, 512, EB, ["ebq"])
         if t == 1:
             quant("qw", "w", 0, "wt", 0, 256, ["wt"], ["w"])
+        if t:
+            pick_out(t - 1)
+            products(t - 1)
         WIN = ["land" + win, win + ".tq", win + ".ts", win + ".cq", win + ".cs", "offv"]
         op("V", "vinq", lambda e: e.tensor_copy(w32(T.vinq[:, 0:80]), w32(T[win + "q"][:, 0:144]).indirect(T.offv[:, 0:5])), r=WIN, w=["vin.q"])
         op("A", "vins", lambda e: e.activation(T.vins[:, 0:80], T[win + "s"][:, 0:144].indirect(T.offv[:, 0:5]), AF.Copy), r=WIN, w=["vin.s"])
         for b in range(4):
             mm("dec%d" % b, 4 + b, "eb", 128 * b, "vin", 0, 128, ["ebq", "vin.q", "vin.s"])
         for b in range(4):
-            op("V", "rec%d" % b, lambda e, b=b: e.tensor_tensor_scan(T["rec%d" % b][:], T.fac[:], ps(4 + b, 0, 80), 0.0, ALU.mult, ALU.add),
-               r=["B%d" % (4 + b), "fac0", "fac1"], w=["rec%d" % b])
-            acopy("cast%d" % b, T.h[:, 64 * (t + 1) + b:64 * (t + 2):4], T["rec%d" % b][:, 4:80:5], ["rec%d" % b], ["h%d" % b], scale=0.5)
-        quant("qv", "v", 0, "h", 0, 128, HT + ["hu"], ["v"])
-        zmul()
+            op("V", "rec%d" % b, lambda e, b=b: e.tensor_tensor_scan(T.h[:, b:4 * NV:4], T.fac[:], ps(4 + b, 0, NV), 0.0, ALU.mult, ALU.add),
+               r=["B%d" % (4 + b), "fac0", "fac1"], w=["h%d" % b])
+        v = "v%d" % t
+        quant("qv", v, 0, "h", 0, 128, HT + ["hu", "hc0", "hc1"], [v])
+        zmul(v)
 
     for t in range(R):
         one_round(t)
 
     n = R * M
-    load("S", "st_oc", T.oc[:, :], u8(T.vq[:, 16:16 + n]), r=["v"], w=["out.oc"])
-    for k in range(4):
-        load("A" if k % 2 else "S", "st_osc%d" % k, T.osc[4 * k:4 * k + 4, :], T.vs[32 * k:32 * k + 4, 16:16 + n], r=["v"], w=["out.osc%d" % k])
+    pick_out(R - 1)
     marks(R, 0)
     marks(R, 1)
     turn(R)
-    for o in range(O):
-        mm("y%d" % o, 6 + o, "w", 128 * o, "v", 0, 128, ["w", "v"])
-    acopy("yc0", T.yt[:, 0:n], ps(6, 16, 16 + n), ["B6"], ["yt0"])
-    vcopy("yc1", T.yt[:, n:2 * n], ps(7, 16, 16 + n), ["B7"], ["yt1"])
-    load("S", "st_y", T.y[:, :], T.yt[:], r=["yt0", "yt1"], w=["out.y"])
+    load("S", "st_oc", T.oc[:, :], u8(T.voq[:, 0:n]), r=["vo.q%d" % t for t in range(R)], w=["out.oc"])
+    for k in range(4):
+        load("A" if k % 2 else "S", "st_osc%d" % k, T.osc[4 * k:4 * k + 4, :], T.vos[32 * k:32 * k + 4, 0:n], r=["vo.s%d" % t for t in range(R)], w=["out.osc%d" % k])
+    products(R - 1)
+    load("S", "st_y", T.y[:, :], T.yt[:], r=["yt%d%d" % (t, o) for t in range(R) for o in range(O)], w=["out.y"])
     for a in range(4):
-        load("A" if a % 2 else "S", "st_mk%d" % a, T.mk[0:1, 64 * a:64 * a + 64], T["mt%d" % R][32 * a:32 * a + 1, :], r=["mt%d" % R], w=["out.mk%d" % a])
+        load("A" if a % 2 else "S", "st_mk%d" % a, T.mk[0:1, 64 * a:64 * a + 64], T["mt%d" % (R % 2)][32 * a:32 * a + 1, :], r=["mt%d" % (R % 2)], w=["out.mk%d" % a])
     op("S", "end", None, r=["out.sel", "out.oc", "out.y"] + ["out.osc%d" % k for k in range(4)] + ["out.mk%d" % a for a in range(4)])
     _emit(P, g, T)
     g.wait_ge(T.sem.ls, sent[0])

from concourse.bass import DstId, RemoteDMATransfer
from concourse.mybir import dt, AluOpType as ALU, AxisListType, ActivationFunctionType as AF

M, R, O = 16, 3, 2
BFT, F32, I32, U16, COD, PLN = "bfloat16", "float32", "int32", "uint16", "float8_e4m3fn_x4", "uint8"
SCRATCH = {}


def _sb(name, n, d):
    SCRATCH[name] = ("sbuf", [128, n], d)


def _codes(name, n):
    _sb(name + "q", n, COD)
    _sb(name + "s", n, PLN)


for _n, _w in (("ctile", 512), ("zt", 512), ("xt", 1024), ("xu", 1024), ("wt", 1024), ("h", 512), ("ind", 512), ("tab", 2048),
               ("kt", 1024), ("oh", 512), ("ohn", 512), ("nm", 520), ("eb", 2048), ("wgt", 512), ("gmask", 8),
               ("ones", 128), ("ident", 128), ("place", 128), ("placen", 16), ("sg", 128), ("junk0", 256), ("junk1", 256)):
    _sb(_n, _w, BFT)
for _n, _w in (("mrow", 256), ("d0", 256), ("d1", 256), ("run0", 256), ("run1", 256), ("kcol", 2), ("cap", 2), ("o16", 2),
               ("tot", 2), ("md", 3), ("step", 7), ("fac", 80), ("low", 16), ("sq", 128),
               ("vrow", 80), ("vblk", 160), ("vtr", 160), ("yt", 96), ("selrow", 48), ("name", 2), ("won", 2)):
    _sb(_n, _w, F32)
for _t in range(R):
    _sb("rk%d" % _t, 2, F32)
for _t in range(2):
    _sb("mk%d" % _t, 96, F32)
    _sb("mt%d" % _t, 64, F32)
for _n, _w in (("pn", 2), ("pl", 2), ("ph", 2), ("vi", 80), ("vi2", 80), ("v16", 16)):
    _sb(_n, _w, I32)
_sb("offv", 6, U16)
_sb("offk", 16, U16)
_sb("offo", 2, U16)
for _t in range(R):
    _sb("off%d" % _t, 4, U16)
    _sb("cnt%d" % _t, 2, BFT)
    _sb("land%d" % _t, 14, BFT)
    _codes("win%d" % _t, 144)
    _codes("v%d" % _t, 128)
for _n, _w in (("c", 128), ("call", 256), ("x", 256), ("xu", 256), ("w", 256), ("vu", 128), ("vo", 48), ("ind", 128), ("kt", 256),
               ("oh", 128), ("ohn", 128), ("nm", 130), ("eb", 512), ("wgt", 128), ("vin", 128)):
    _codes(_n, _w)
for _b in range(8):
    SCRATCH["ps%d" % _b] = ("psum", [128, 512], F32)
SEMAPHORES = ["rc"] + ["rn%d" % t for t in range(R)] + ["rt%d" % t for t in range(R)] + ["ls"] + ["e%d" % i for i in range(140)]


def _add(P, q, name, fn, r=(), w=(), inc=1, ext=None):
    ops, tags = P["ops"], P["tags"]
    i = len(ops)
    deps = set()
    if q == "G" and name[:3] != "snd":
        w = list(w) + ["pool"]
    for t in r:
        s = tags.setdefault(t, {"w": None, "r": []})
        if s["w"] is not None:
            deps.add(s["w"])
        if t[0] == "B":
            deps.update(j for j in s["r"] if ops[j]["q"] != q)
    for t in w:
        s = tags.setdefault(t, {"w": None, "r": []})
        if s["w"] is not None:
            deps.add(s["w"])
        deps.update(s["r"])
    for t in r:
        tags[t]["r"].append(i)
    for t in w:
        tags[t]["w"] = i
        tags[t]["r"] = []
    deps.discard(i)
    ops.append({"q": q, "name": name, "fn": fn, "deps": deps, "inc": inc, "ext": ext})


def _emit(P, g, T):
    queues = {"G": g, "V": g.vector, "A": g.scalar, "P": g.tensor, "S": g.sync}
    ops = P["ops"]
    known = {q: 0 for q in queues}
    done, waits, used = [], [], set()
    for i, o in enumerate(ops):
        if o["ext"] is not None:
            done.append(1 << i)
            waits.append([])
            continue
        need = []
        for j in sorted(o["deps"], reverse=True):
            if not known[o["q"]] >> j & 1:
                need.append(j)
                known[o["q"]] |= done[j]
        keep = [j for j in need if not any(done[m] >> j & 1 for m in need if m != j)]
        waits.append(sorted(keep))
        used.update(keep)
        done.append(known[o["q"]] | 1 << i)
    pool, val = [], {}
    for i, o in enumerate(ops):
        if o["ext"] is not None:
            val[i] = o["ext"]
            continue
        q = queues[o["q"]]
        for j in waits[i]:
            q.wait_ge(*val[j])
        if o["fn"] is None:
            continue
        ins = o["fn"](q)
        if i in used:
            dma = o["inc"] > 1
            free = [s for s in pool if not dma and not s["dma"] and done[i] >> s["last"] & 1]
            free.sort(key=lambda s: -s["last"])
            if free:
                s = free[0]
            else:
                s = {"sem": T.sem["e%d" % len(pool)], "n": 0, "dma": dma}
                pool.append(s)
            s["last"] = i
            s["n"] += o["inc"]
            ins.then_inc(s["sem"], o["inc"])
            val[i] = (s["sem"], s["n"])


def rank_program(g, core, T, topo):
    r = T.rank_of(core)
    if r is None:
        return
    cores = list(T.cores)
    N = len(cores)
    P = {"ops": [], "tags": {}}
    chip = [topo.chip(q) for q in cores]
    ways = {"far": [], "plane": [], "mate": []}
    for d in range(1, N):
        q = r ^ d
        way = "mate" if topo.mates(chip[r], chip[q]) else "plane" if topo.same_plane(chip[r], chip[q]) else "far"
        ways[way].append(q)
    others = []
    while ways["far"] or ways["plane"]:
        for way in ("far", "plane"):
            others += ways[way][:1]
            del ways[way][:1]
    others += ways["mate"]
    mask = 0xFFFF
    for q in others:
        mask &= topo.mask(core, cores[q])
    lanes = len([e for e in topo.engines(core, cores[others[0]]) if mask >> e & 1])
    sent = [0]

    def op(*a, **k):
        _add(P, *a, **k)

    def u8(ap):
        return ap.bitcast(dt.uint8)

    def w32(ap):
        return ap.bitcast(dt.uint32)

    def slot(src, dst):
        return (src - dst) % N

    def send(name, reads, src, dst, sem):
        ids = []
        for q in others:
            rid, pid, _ = topo.addr(cores[q])
            ids.append(DstId(rid=rid, pnc=pid))
        dsts = [dst(q) for q in others]
        sent[0] += lanes
        op("G", name, lambda e: e.remote_dma_fused([RemoteDMATransfer(dst_ids=ids, dma_engine_mask=mask, remote_sem=T.sem[sem],
                                                                      srcs=[src], dsts=dsts)], local_sem=T.sem.ls), r=reads)

    def memset(name, ap, v, w):
        op("V", name, lambda e: e.memset(ap, v), w=w)

    def quant(name, out, c0, tile, a, n, r, w):
        op("V", name, lambda e: e.quantize_mx(T[out + "q"][:, c0:c0 + n], T[out + "s"][:, c0:c0 + n], T[tile][:, a:a + 4 * n]), r=r, w=w)

    def mm(name, bank, st, a, mv, b, n, r, start=True, stop=True):
        op("P", name, lambda e: e.matmul_mx(T["ps%d" % bank][:, 0:n], T[st + "q"][:, a:a + 128], T[st + "s"][:, a:a + 128],
                                            T[mv + "q"][:, b:b + n], T[mv + "s"][:, b:b + n], start, stop), r=r, w=["B%d" % bank])

    def ps(bank, a, b):
        return T["ps%d" % bank][:, a:b]

    def ts(name, out, in0, s1, s2, o0, o1, r, w):
        if o1 is None:
            op("V", name, lambda e: e.tensor_scalar(out, in0, s1, None, o0), r=r, w=w)
        else:
            op("V", name, lambda e: e.tensor_scalar(out, in0, s1, s2, o0, o1), r=r, w=w)

    def tt(name, out, in0, in1, o, r, w):
        op("V", name, lambda e: e.tensor_tensor(out, in0, in1, o), r=r, w=w)

    def vcopy(name, out, in_, r, w):
        op("V", name, lambda e: e.tensor_copy(out, in_), r=r, w=w)

    def acopy(name, out, in_, r, w, **k):
        op("A", name, lambda e: e.activation(out, in_, AF.Copy, **k), r=r, w=w)

    def load(q, name, out, in_, r=(), w=()):
        op(q, name, lambda e: e.dma_start(out, in_), r=r, w=w, inc=16)

    order = [None] * M
    for k in range(M):
        i, h = (r - k) % N, k // N
        order[(i % 4) + 4 * h + 8 * (i // 4)] = k
    place_of = {k: j for j, k in enumerate(order)}
    HT = ["h0", "h1", "h2", "h3"]
    EB = ["eb0", "eb1", "eb2", "eb3"]
    PL = ["place%d" % j for j in range(M)]
    RND = 1.5 * 2.0 ** 27
    CV = 96
    NV = 5 * M

    load("S", "ldc", T.ctile[:, 0:128], T.c[:, :], w=["ctile"])
    load("A", "ldx", T.xt[:, :], T.x[:, :], w=["xt"])
    memset("ms_c", T.ctile[:, 128:512], 0.0, ["ctile0"])
    memset("ms_ones", T.ones[:], 1.0, ["ones"])
    memset("ms_h", T.h[:], 0.0, HT + ["hu", "hc0", "hc1"])
    memset("ms_h1", T.h[:, 4 * CV:4 * CV + 2], 1.0, ["hc0"])
    memset("ms_h2", T.h[:, 4 * CV + 6:4 * CV + 8], 1.0, ["hc1"])
    load("S", "ldu", T.h[:, 4 * NV:4 * NV + 4], T.u[:, 0:4], w=["hu"])
    memset("ms_zt", T.zt[:], 0.0, ["zt"])
    op("G", "pn", lambda e: e.iota(T.pn[:], [[128, 2]], 0, 1), w=["pn"])
    op("G", "vi", lambda e: e.iota(T.vi[:], [[4, 2], [16, 8], [17, 5]], 256 - 17 - 16 * r, 0), w=["vi"])
    op("G", "v16", lambda e: e.iota(T.v16[:], [[1, 16]], 0, 0), w=["v16"])
    op("G", "ident", lambda e: e.affine_select(T.ident[:], T.ones[:], [[-1, 128]], ALU.is_equal, 0.0, 0, 1), r=["ones"], w=["ident"])

    quant("qc", "c", 0, "ctile", 0, 128, ["ctile", "ctile0"], ["c"])
    send("snd_cq", ["c"], u8(T.cq[:, 0:32]), lambda q: u8(T.callq[:, 32 * r:32 * r + 32]), "rc")
    send("snd_cs", ["c"], T.cs[:, 0:32], lambda q: T.calls[:, 32 * r:32 * r + 32], "rc")
    load("S", "ownq", u8(T.callq[:, 32 * r:32 * r + 32]), u8(T.cq[:, 0:32]), r=["c"], w=["own.q"])
    load("S", "owns", T.calls[:, 32 * r:32 * r + 32], T.cs[:, 0:32], r=["c"], w=["own.s"])
    op("X", "arr_c", None, w=["call"], ext=(T.sem.rc, 2 * lanes * (N - 1)))
    CALL = ["call", "own.q", "own.s"]

    for j in range(M):
        acopy("place", T.place[:, j:128:16], T.ones[:, 0:8], ["ones"], [PL[j]], scale=255.0 - 2.0 * order[j])
    memset("ms_kt", T.kt[:], 0.0, ["kta", "ktb", "kto0", "kto1", "ktr0", "ktr1", "ktc", "ktd"])
    for t in range(2):
        memset("ms_mk%d" % t, T["mk%d" % t][:, 32:96], 0.0, ["mk%d.0" % t, "mk%d.1" % t])
    for a in range(4):
        for b in range(2):
            (vcopy if b else acopy)("xu", T.xu[:, 512 * b + 128 * a:512 * b + 128 * a + 128], T.xt[:, 256 * a + 128 * b:256 * a + 128 * b + 128],
                                    ["xt"], ["xu%d%d" % (a, b)])
    quant("qv", "vu", 0, "h", 0, 128, HT + ["hu", "hc0", "hc1"], ["vu"])
    quant("qxu", "xu", 0, "xu", 0, 256, ["xu%d%d" % (a, b) for a in range(4) for b in range(2)], ["xuq"])
    acopy("z_nm", T.nm[:, 0:512], T.zt[:], ["zt"], ["nm", "nmlo", "nmhi"])
    acopy("z_oh", T.oh[:], T.zt[:], ["zt"], ["oh0", "oh1"])
    ts("pl", T.pl[:], T.pn[:], 15, None, ALU.bitwise_and, None, ["pn"], ["pl"])
    ts("vi2", T.vi2[:], T.vi[:], 127, None, ALU.bitwise_and, None, ["vi"], ["vi2"])
    for d in range(3):
        ts("md", T.md[:, d:d + 1], T.pl[:, 0:1], 3.0 + d, None, ALU.is_equal, None, ["pl"], ["md%d" % d])
    vcopy("vrow", T.vrow[:], T.vi2[:], ["vi2"], ["vrow"])
    for k in range(7):
        acopy("step", T.step[:, k:k + 1], T.md[:, 1 + k // 4:2 + k // 4], ["md%d" % (1 + k // 4)], ["step%d" % k], scale=16.0 * 2 ** k)
    quant("qx", "x", 0, "xt", 0, 256, ["xt"], ["x"])
    memset("ms_wgt", T.wgt[:], 256.0, ["wgt"])
    memset("ms_wgt", T.wgt[:, 2:512:4], 1.0, ["wgt"])
    op("G", "ktc", lambda e: e.iota(T.kt[32:33, 2:1024:4], [[0, 16], [-1, 16]], 15, 0, allow_small_or_imprecise_dtypes=True), w=["ktc", "ktc2"])
    op("G", "ktd", lambda e: e.iota(T.kt[64:65, 2:1024:4], [[-16, 16], [0, 16]], 240, 0, allow_small_or_imprecise_dtypes=True),
       w=["ktd", "ktd2", "ktd3"])
    op("G", "gmask0", lambda e: e.affine_select(T.gmask[:], T.ones[:, 0:8], [[-16, 8]], ALU.is_ge, 0.0, 0, 1), r=["ones"], w=["gmask"])
    op("G", "gmask1", lambda e: e.affine_select(T.gmask[:], T.gmask[:], [[16, 8]], ALU.is_ge, 0.0, 15, -1), r=["gmask"], w=["gmask"])

    def zmul(v):
        for b in range(2):
            mm("z%d" % b, 4 + b, "xu", 128 * b, v, 0, 128, ["xuq", v])

    def mk(t, b):
        return T["mk%d" % (t % 2)][:, 32 * b + 32:32 * b + 33]

    def marks(t, b):
        q = "mk%d.%d" % (t % 2, b)
        if t == 0:
            vcopy("mark%d" % b, mk(0, b), ps(4 + b, NV, NV + 1), ["B%d" % (4 + b)], [q])
        else:
            op("V", "mark%d" % b, lambda e: e.tensor_tensor_scan(T["mk%d" % (t % 2)][:, 32 * b + 33 - M:32 * b + 33], T["ps%d" % (4 + b)][:, 4:NV:5],
                                                                 T.low[:], mk(t - 1, b), ALU.max, ALU.max),
               r=["B%d" % (4 + b), "low", "mk%d.%d" % ((t - 1) % 2, b)], w=[q])

    def turn(t):
        op("V", "turn", lambda e: e.transpose(T["mt%d" % (t % 2)][:], T["mk%d" % (t % 2)][:, 32:96]),
           r=["mk%d.0" % (t % 2), "mk%d.1" % (t % 2)], w=["mt%d" % (t % 2)])

    def spread(t, aa):
        for a in aa:
            op("G", "spread%d" % a, lambda e, a=a: e.partition_broadcast(T.mrow[:, 64 * a:64 * a + 64], T["mt%d" % (t % 2)][32 * a:32 * a + 1, :], 128),
               r=["mt%d" % (t % 2)], w=["mrow%d" % a])

    zmul("vu")
    marks(0, 0)
    marks(0, 1)
    quant("qwgt", "wgt", 0, "wgt", 0, 128, ["wgt"], ["wgtq"])
    turn(0)
    spread(0, (0, 1, 2, 3))
    ts("tab", T.tab[:, 0:16], T.v16[:], T.md[:, 0:1], None, ALU.mult, None, ["v16", "md0"], ["tab0"])
    memset("ms_cap", T.cap[:], 256.0, ["cap"])
    for k in range(5):
        m = 16 << k
        ts("tab", T.tab[:, m:2 * m], T.tab[:, 0:m], T.step[:, k:k + 1], None, ALU.add, None, ["tab%d" % j for j in range(k + 1)] + ["step%d" % k], ["tab%d" % (k + 1)])
    TOP = 256 * (N - 1) + 16
    TAB = ["tab%d" % j for j in range(8)]
    memset("kt32", T.kt[32:33, 130:1024:512], 0.0, ["ktc"])
    memset("kt96", T.kt[96:97, 130:1024:512], 15.0, ["ktc2"])
    memset("kt64", T.kt[64:65, 258:1024:512], 0.0, ["ktd"])
    memset("kt96", T.kt[96:97, 258:259], 176.0, ["ktd2"])
    memset("kt96", T.kt[96:97, 770:771], 48.0, ["ktd3"])
    for k in range(M):
        acopy("vrowk", T.vrow[:, 5 * k:5 * k + 1], T.ones[:, 0:1], ["vrow", "ones"], ["vrow.%d" % k], scale=float(128 + place_of[k]))
    for k in (5, 6):
        op("A", "tab", lambda e, m=16 << k, k=k: e.activation(T.tab[:, m:min(2 * m, TOP)], T.tab[:, 0:min(m, TOP - m)], AF.Identity, bias=T.step[:, k:k + 1]),
           r=["tab%d" % j for j in range(k + 1)] + ["step%d" % k], w=["tab%d" % (k + 1)])

    def above(t, b, k):
        ts("above", T.ind[:, 2 * k + b:512:4], ps(b, 128 * k, 128 * k + 128), mk(t, b), None, ALU.is_gt, None,
           ["B%d" % b, "mk%d.%d" % (t % 2, b)], ["ind%d%d" % (b, k)])

    def above_a(t):
        op("A", "sgn", lambda e: e.activation(T.sg[:], T.sq[:], AF.Sign, bias=mk(t, 0), scale=-1.0), r=["sq", "mk%d.0" % (t % 2)], w=["sg"])
        op("A", "neg", lambda e: e.activation(T.ind[:, 2:512:4], T.sg[:], AF.Relu, scale=-1.0), r=["sg"], w=["ind01"])

    def pieces(what, b, lo, hi):
        return ["%s%d.%d" % (what, b, h) for h in range(lo // 64, hi // 64)]

    def name_diff(b, lo, hi):
        tt("diff%d" % b, T["d%d" % b][:, lo:hi], ps(2 + b, lo, hi), T.mrow[:, lo:hi], ALU.subtract,
           ["B%d" % (2 + b)] + ["mrow%d" % a for a in range(lo // 64, hi // 64)], pieces("d", b, lo, hi))

    def name_run(b, lo, hi):
        first = T["run%d" % b][:, lo - 1:lo] if lo else -1e29
        op("V", "run%d" % b, lambda e: e.tensor_tensor_scan(T["run%d" % b][:, lo:hi], T["d%d" % b][:, lo:hi], T["d%d" % b][:, lo:hi], first, ALU.max, ALU.max),
           r=pieces("d", b, lo, hi) + (pieces("run", b, 0, lo) if lo else []), w=pieces("run", b, lo, hi))

    def name_at(b):
        op("A", "name%d" % b, lambda e: e.activation(T["junk%d" % b][:], T["run%d" % b][:], AF.Sign, bias=T["run%d" % b][:, 255:256], scale=-1.0,
                                                     accum_out=T.name[:, b:b + 1]), r=pieces("run", b, 0, 256), w=["junk%d" % b, "name%d" % b])

    def pick_out(t):
        v = "v%d" % t
        op("V", "outq", lambda e: e.tensor_copy(w32(T.voq[:, M * t:M * t + M]), w32(T[v + "q"][:, 0:128]).indirect(T.offo[:, 0:1])), r=[v, "offo"], w=["vo.q%d" % t])
        op("A", "outs", lambda e: e.activation(T.vos[:, M * t:M * t + M], T[v + "s"][:, 0:128].indirect(T.offo[:, 0:1]), AF.Copy), r=[v, "offo"], w=["vo.s%d" % t])

    def products(t):
        v = "v%d" % t
        for o in range(O):
            mm("y%d" % o, 6 + o, "w", 128 * o, v, 0, 128, ["w", v])
        for o in range(O):
            (vcopy if o else acopy)("yc%d" % o, T.yt[:, R * M * o + M * t:R * M * o + M * t + M], T["ps%d" % (6 + o)][:, 4:NV:5],
                                    ["B%d" % (6 + o)], ["yt%d%d" % (t, o)])

    def one_round(t):
        win, off, rk, cnt, land = "win%d" % t, "off%d" % t, "rk%d" % t, "cnt%d" % t, "land%d" % t
        if t == 0:
            for b in range(2):
                mm("sb%d" % b, b, "xu", 128 * b, "call", 0, 256, ["xuq"] + CALL)
            for b in range(2):
                for k in range(2):
                    above(t, b, k)
        else:
            marks(t, 0)
            above_a(t)
            above(t, 0, 0)
            marks(t, 1)
            turn(t)
            above(t, 1, 0)
            above(t, 1, 1)
        quant("qind", "ind", 0, "ind", 0, 128, ["ind00", "ind01", "ind10", "ind11"], ["indq"])
        if t:
            spread(t, (0, 1))
        mm("cnt", 6, "ind", 0, "vu", 0, 128, ["indq", "vu"])
        vcopy("cnt", T[cnt][:], ps(6, CV, CV + 2), ["B6"], [cnt])
        send("snd_n", [cnt], T[cnt][:], lambda q: T[land][:, 2 * slot(r, q) - 2:2 * slot(r, q)], "rn%d" % t)
        op("X", "arr_n", None, w=[land], ext=(T.sem["rn%d" % t], lanes * (N - 1)))
        ts("c16", T.o16[:], ps(6, CV, CV + 2), RND, RND, ALU.add, ALU.subtract, ["B6"], ["o16"])
        tt("crest", T.won[:], ps(6, CV, CV + 2), T.o16[:], ALU.subtract, ["B6", "o16"], ["won"])
        tt("ccap", T.o16[:], T.o16[:], T.cap[:], ALU.min, ["cap", "o16"], ["o16"])
        for b in range(2):
            acopy("own", T.kt[:, 512 * b + 3:512 * b + 512:4], T.ident[:], ["ident", "won"], ["ktr%d" % b], scale=T.won[:, b:b + 1])
            acopy("own", T.kt[:, 512 * b + 1:512 * b + 512:4], T.ident[:], ["ident", "o16"], ["kto%d" % b], scale=T.o16[:, b:b + 1])
        if t:
            spread(t, (2, 3))
        else:
            op("G", "placen", lambda e: e.iota(T.placen[:], [[-2, 16]], 255, 0, allow_small_or_imprecise_dtypes=True), w=["placen"])
            for b in range(2):
                mm("sa%d" % b, 2 + b, "call", 128 * b, "x", 0, 256, ["x"] + CALL)
        for lo, hi in (((0, 128), (128, 192), (192, 256)) if t else ((0, 256),)):
            for b in range(2):
                name_diff(b, lo, hi)
            for b in range(2):
                name_run(b, lo, hi)
        name_at(0)
        if t == 0:
            for b in range(4):
                load("S", "z_eb", T.eb[:, 512 * b:512 * b + 512], T.zt[:], r=["zt", land], w=[EB[b]])
        if t == 1:
            load("S", "ldw", T.wt[:, :], T.w[:, :], r=[land], w=["wt"])
            load("S", "z_ohn", T.ohn[:], T.zt[:], r=["zt", land], w=["ohn"])
        for b in range(2):
            op("V", "tot", lambda e, b=b: e.tensor_reduce(T.tot[:, b:b + 1], T[land][:, b:14:2], AxisListType.X, ALU.add), r=[land], w=["tot%d" % b])
        for b in range(2):
            ts("offk", T.offk[:, 8 * b:8 * b + 8], T.gmask[:], T.tot[:, b:b + 1], None, ALU.mult, None, ["gmask", "tot%d" % b], ["offk%d" % b])
        op("A", "gain1", lambda e: e.activation(T.kt[:, 512:1024:4], T.tab[:, 0:TOP].indirect(T.offk[:, 8:16]), AF.Copy), r=TAB + ["offk1"], w=["ktb"])
        op("V", "gain0", lambda e: e.tensor_copy(T.kt[:, 0:512:4], T.tab[:, 0:TOP].indirect(T.offk[:, 0:8])), r=TAB + ["offk0"], w=["kta"])
        name_at(1)
        KC = ["ktc", "ktd", "ktc2", "ktd2", "ktd3"]
        quant("qkta", "kt", 0, "kt", 0, 128, ["kta", "kto0", "ktr0"] + KC, ["ktqa"])
        quant("qktb", "kt", 128, "kt", 512, 128, ["ktb", "kto1", "ktr1"] + KC, ["ktqb"])
        mm("kcol0", 6, "kt", 0, "wgt", 0, 128, ["ktqa", "wgtq"])
        mm("krow", 7, "wgt", 0, "kt", 0, 256, ["ktqa", "ktqb", "wgtq"])
        mm("kcol1", 4, "kt", 128, "wgt", 0, 128, ["ktqb", "wgtq"])
        if t == 0:
            ts("ph", T.ph[:], T.pn[:], 240, None, ALU.bitwise_and, None, ["pn"], ["ph"])
            vcopy("nm_l", T.nm[:, 0:2], T.pl[:], ["pl", "nm"], ["nm_l"])
        vcopy("kcc0", T.kcol[:, 0:1], ps(6, 0, 1), ["B6"], ["kcol0"])
        if t == 0:
            vcopy("nm_h", T.nm[:, 8:10], T.ph[:], ["ph", "nm"], ["nm_h"])
            memset("z_nm2", T.nm[:, 512:520], 0.0, ["nm2"])
        ts("n16", T.nm[:, 24:26], T.name[:], RND, RND, ALU.add, ALU.subtract, ["name0", "name1", "nm"], ["nmhi"])
        vcopy("kcc1", T.kcol[:, 1:2], ps(4, 0, 1), ["B4"], ["kcol1"])
        tt("nrest", T.nm[:, 16:18], T.name[:], T.nm[:, 24:26], ALU.subtract, ["name0", "name1", "nmhi", "nm"], ["nmlo"])
        quant("qnm", "nm", 0, "nm", 0, 130, ["nm", "nm2", "nm_l", "nm_h", "nmlo", "nmhi"], ["nmq"])
        for b in range(2):
            op("A", "rank%d" % b, lambda e, b=b: e.activation(T["junk%d" % b][:], ps(7, 0, 256), AF.Sign, bias=T.kcol[:, b:b + 1], scale=-1.0,
                                                              accum_out=T[rk][:, b:b + 1]), r=["B7", "kcol%d" % b], w=["junk%d" % b, "%s.%d" % (rk, b)])
        for b in range(2):
            ts("onehot%d" % b, T.oh[:, b:512:4], T.place[:], T[rk][:, b:b + 1], None, ALU.is_equal, None, [rk + ".%d" % b] + PL, ["oh%d" % b])
        quant("qoh", "oh", 0, "oh", 0, 128, ["oh0", "oh1"], ["ohq"])
        mm("lists", 5, "oh", 0, "nm", 0, 128, ["ohq", "nmq"])
        ts("offt", T[off][:, 0:1], ps(5, 4, 5), ps(5, 6, 7), None, ALU.add, None, ["B5"], [off + "t"])
        op("V", "tokq", lambda e: e.tensor_copy(w32(T[win + "q"][:, 0:16]), w32(T.xq[:, 0:256]).indirect(T[off][:, 0:1])), r=["x", off + "t"], w=[win + ".tq"])
        op("A", "toks", lambda e: e.activation(T[win + "s"][:, 0:16], T.xs[:, 0:256].indirect(T[off][:, 0:1]), AF.Copy), r=["x", off + "t"], w=[win + ".ts"])
        send("snd_tq", [win + ".tq"], u8(T[win + "q"][:, 0:8]), lambda q: u8(T[win + "q"][:, 16 * slot(r, q):16 * slot(r, q) + 8]), "rt%d" % t)
        send("snd_ts", [win + ".ts"], T[win + "s"][:, 0:8], lambda q: T[win + "s"][:, 16 * slot(r, q):16 * slot(r, q) + 8], "rt%d" % t)
        op("X", "arr_t", None, w=["land" + win], ext=(T.sem["rt%d" % t], 2 * lanes * (N - 1)))
        ts("offc", T[off][:, 2:3], ps(5, 0, 1), ps(5, 2, 3), None, ALU.add, None, ["B5"], [off + "c"])
        op("V", "candq", lambda e: e.tensor_copy(w32(T[win + "q"][:, 128:144]), w32(T.callq[:, 0:256]).indirect(T[off][:, 2:3])), r=CALL + [off + "c"], w=[win + ".cq"])
        op("A", "cands", lambda e: e.activation(T[win + "s"][:, 128:144], T.calls[:, 0:256].indirect(T[off][:, 2:3]), AF.Copy), r=CALL + [off + "c"], w=[win + ".cs"])
        if t + 1 < R:
            ts("won", T.won[:], T[rk][:], 224.0, -4352.0, ALU.is_gt, ALU.mult, [rk + ".0", rk + ".1"], ["won"])
            ts("won", T.won[:], T.won[:], 256.0, None, ALU.add, None, ["won"], ["won"])
            tt("cap", T.cap[:], T.cap[:], T.won[:], ALU.min, ["won", "cap"], ["cap"])
        else:
            for s in range(R):
                for b in range(2):
                    rs = "rk%d" % s
                    ts("ohn", T.ohn[:, 64 * s + b:64 * s + 64:4], T.placen[:], T[rs][:, b:b + 1], None, ALU.is_equal, None,
                       ["ohn", "placen", rs + ".%d" % b], ["ohn%d%d" % (s, b)])
            quant("qohn", "ohn", 0, "ohn", 0, 128, ["ohn"] + ["ohn%d%d" % (s, b) for s in range(R) for b in range(2)], ["ohnq"])
            mm("sel0", 6, "nm", 0, "ohn", 0, 128, ["nmq", "ohnq"], True, False)
            mm("sel1", 6, "nm", 2, "ohn", 0, 128, ["nmq", "ohnq"], False, True)
            acopy("selrow", T.selrow[0:1, :], T.ps6[0:1, 0:48], ["B6"], ["selrow"])
            load("S", "st_sel", T.sel[0:1, :], T.selrow[0:1, :], r=["selrow"], w=["out.sel"])
        if t == 0:
            for c in range(5):
                for b in range(2):
                    acopy("vblk", T.vblk[:, 32 * c + 16 * b:32 * c + 16 * b + 16], T.vrow[:, 16 * c:16 * c + 16],
                          ["vrow"] + ["vrow.%d" % k for k in range(M)], ["vblk%d%d" % (c, b)])
            for b in range(4):
                acopy("eb", T.eb[:, 512 * b + b:512 * b + 512:4], T.ident[:], ["ident"], [EB[b]], scale=0.5)
            acopy("sq", T.sq[:], ps(0, 128, 256), ["B0"], ["sq"])
            quant("qzv", "vin", 0, "zt", 0, 128, ["zt"], ["vin.q", "vin.s"])
            memset("ms_low", T.low[:], -1e29, ["low"])
            memset("ms_fac", T.fac[:], 0.5, ["fac0", "fac1"])
            ts("offo", T.offo[:], T.pl[:], 5.0, 4.0, ALU.mult, ALU.add, ["pl"], ["offo"])
            memset("ms_fac0", T.fac[:, 0:80:5], 0.0, ["fac0"])
            memset("ms_fac1", T.fac[:, 1:80:5], 1.0, ["fac1"])
            op("V", "vtr", lambda e: e.transpose(T.vtr[:], T.vblk[:]), r=["vblk%d%d" % (c, b) for c in range(5) for b in range(2)], w=["vtr"])
            vcopy("offv", T.offv[:, 0:5], T.vtr[:, 0:160:32], ["vtr"], ["offv"])
            quant("qeb", "eb", 0, "eb", 0, 512, EB, ["ebq"])
        if t == 1:
            quant("qw", "w", 0, "wt", 0, 256, ["wt"], ["w"])
        if t:
            pick_out(t - 1)
            products(t - 1)
        WIN = ["land" + win, win + ".tq", win + ".ts", win + ".cq", win + ".cs", "offv"]
        op("V", "vinq", lambda e: e.tensor_copy(w32(T.vinq[:, 0:80]), w32(T[win + "q"][:, 0:144]).indirect(T.offv[:, 0:5])), r=WIN, w=["vin.q"])
        op("A", "vins", lambda e: e.activation(T.vins[:, 0:80], T[win + "s"][:, 0:144].indirect(T.offv[:, 0:5]), AF.Copy), r=WIN, w=["vin.s"])
        for b in range(4):
            mm("dec%d" % b, 4 + b, "eb", 128 * b, "vin", 0, 128, ["ebq", "vin.q", "vin.s"])
        for b in range(4):
            op("V", "rec%d" % b, lambda e, b=b: e.tensor_tensor_scan(T.h[:, b:4 * NV:4], T.fac[:], ps(4 + b, 0, NV), 0.0, ALU.mult, ALU.add),
               r=["B%d" % (4 + b), "fac0", "fac1"], w=["h%d" % b])
        v = "v%d" % t
        quant("qv", v, 0, "h", 0, 128, HT + ["hu", "hc0", "hc1"], [v])
        zmul(v)

    for t in range(R):
        one_round(t)

    n = R * M
    pick_out(R - 1)
    marks(R, 0)
    marks(R, 1)
    turn(R)
    load("S", "st_oc", T.oc[:, :], u8(T.voq[:, 0:n]), r=["vo.q%d" % t for t in range(R)], w=["out.oc"])
    for k in range(4):
        load("A" if k % 2 else "S", "st_osc%d" % k, T.osc[4 * k:4 * k + 4, :], T.vos[32 * k:32 * k + 4, 0:n], r=["vo.s%d" % t for t in range(R)], w=["out.osc%d" % k])
    products(R - 1)
    load("S", "st_y", T.y[:, :], T.yt[:], r=["yt%d%d" % (t, o) for t in range(R) for o in range(O)], w=["out.y"])
    for a in range(4):
        load("A" if a % 2 else "S", "st_mk%d" % a, T.mk[0:1, 64 * a:64 * a + 64], T["mt%d" % (R % 2)][32 * a:32 * a + 1, :], r=["mt%d" % (R % 2)], w=["out.mk%d" % a])
    op("S", "end", None, r=["out.sel", "out.oc", "out.y"] + ["out.osc%d" % k for k in range(4)] + ["out.mk%d" % a for a in range(4)])
    _emit(P, g, T)
    g.wait_ge(T.sem.ls, sent[0])
